import numpy as np, ml_dtypes
CORES = [40,41,42,43,44,45,46,47]
N = 8
BF = ml_dtypes.bfloat16
def gentries(a):
    return np.ascontiguousarray(a.reshape(8, 16, -1).transpose(0, 2, 1)).reshape(8, -1)
def gtable(e):
    e = np.asarray(e); return np.ascontiguousarray(e.reshape(8, -1, 16).transpose(0, 2, 1)).reshape(128, -1).astype(np.int32)
S, K, W, C, RO = 512, 8, 4096, 8, 4
def H(e, v):
    return ((e * v >> 5) + e + 37 * v) & (W - 1)
def U(x, w):
    return np.add.reduce(x * w, axis=-1, dtype=np.int32) & (W - 1)
def applies(d, x, least):
    return np.add.reduce(d > x, axis=-1, dtype=np.int32) >= least
def parts(rng):
    lev = rng.choice(np.array([96, 160, 256]), (N, 8, 1, W))
    d = (rng.random((N, 8, 16, W)) * lev).astype(np.int64)
    return d, rng.integers(0, W, (N, 8, S, K)), rng.integers(0, 256, (N, 8, 16, S)), rng.integers(1, 256, (N, 8, 16))
def pack(d, e, z, w):
    return {"dv": d.reshape(N, 128, W).astype(np.float32).astype(BF), "ef": np.stack([gtable(a.reshape(8, -1)) for a in e]),
            "zv": z.reshape(N, 128, S).astype(np.float32).astype(BF), "wt": w.reshape(N, 128, 1).astype(np.int32)}
def stage(rng, d, w, r, g):
    o = rng.permutation(16); w[r, g] = 1; w[r, g, o[:8]] = 255
    m = np.zeros(16, np.int64); m[o[:4]] = 255; m[o[8:12]] = 255
    q = np.zeros(16, np.int64); q[rng.permutation(o[:15])[:9]] = 255
    row = int(o[15]); one = np.zeros(16, np.int64); one[row] = 255
    d[r, g, :, 0] = m; d[r, g, :, W - 1] = q; d[r, g, :, H(W - 1, 255 * 1024 & (W - 1))] = 255
    d[r, g, :, H(0, 255)] = m + one; d[r, g, :, H(W - 1, 255)] = q + one
    return row
def setup_inputs(rng):
    return pack(*parts(rng))
def setup_inputs_corners(rng):
    d, e, z, w = parts(rng); i = np.arange(S); kk = np.arange(K)
    for r in range(N):
        for g in range(8):
            if (r + g) % 2 == 1:
                stage(rng, d, w, r, g)
                few = np.argsort(np.argsort(rng.random((16, 64)), axis=0), axis=0) < np.where(np.arange(64) % 4 == 1, 0, 7)
                d[r, g, :, 16:80] = few * rng.integers(1, 256, (16, 64))
                goal = rng.choice(np.array([0, 1, 2, K - 2, K - 1]), S)[:, None]
                cold = rng.integers(16, 80, (S, K))
                v = np.where((kk < goal) | (goal == 0), cold, np.where(kk == goal, W - 1, e[r, g])); v[:, 0] = 0
                m = i % 4 != 3
                e[r, g] = np.where(m[:, None], v, e[r, g]); z[r, g] = np.where(m, 0, z[r, g])
            else:
                e[r, g, ::4] = e[r, g, ::4, :1]; e[r, g, 1::4] = (W - 1) * rng.integers(0, 2, e[r, g, 1::4].shape)
                z[r, g, :, 5::8] = 255; z[r, g, :, 6::8] = 0
    return pack(d, e, z, w)
def setup_inputs_ends(rng):
    p = rng.choice(np.array([0.0, 0.25, 0.5, 0.75, 0.9, 1.0]), (N, 8, 1, W)); d = 255 * (rng.random((N, 8, 16, W)) < p).astype(np.int64)
    d[..., 2::4] = rng.integers(0, 256, d[..., 2::4].shape)
    p = rng.choice(np.array([0.0, 0.1, 0.3, 0.5, 1.0]), (N, 8, 1, S)); z = 255 * (rng.random((N, 8, 16, S)) < p).astype(np.int64)
    z[..., 2::5] = rng.integers(0, 256, z[..., 2::5].shape)
    e = (W - 1) * rng.integers(0, 2, (N, 8, S, K)); w = np.where(rng.random((N, 8, 16)) < 0.5, 1, 255)
    for r in range(N):
        for g in range(8):
            if r < 2:
                row = stage(rng, d, w, r, g); z[r, g] = 0; z[r, g, row] = 255 * rng.integers(0, 2, S); z[r, g, row, 0] = 255; z[r, g, row, S - 1] = 0
                e[r, g, :, 0] = 0; e[r, g, :, 1:3] = 2 + 4 * rng.integers(0, W // 4, (S, 2)); e[r, g, :, K - 1] = W - 1
            elif (r == N - 1 and g == 7) or (r == N - 2 and g == 6):
                w[r, g] = 255; z[r, g, :, 1] = 255; z[r, g, :, S - 1] = 255; z[r, g, :, 3] = 0
            else:
                w[r, g, 13:15] = 1; w[r, g, 15] = 255
                for j in (1, S - 1):
                    z[r, g, :, j] = 0; z[r, g, 13:, j] = 255; e[r, g, j, 0] = W - 1; e[r, g, j, K - 1] = W - 1
    z[0, 7, :, S - 1] = 255
    return pack(d, e, z, w)
def setup_inputs_full(rng):
    d, e, z, w = parts(rng); i = np.arange(S); kk = np.arange(K); quiet = int(rng.integers(0, N)); turn = int(rng.integers(0, 8))
    for r in range(N):
        for g in range(8):
            kind = (5, 1, 5, 3)[g % 4] if r == quiet else (g + 3 * r + turn) % 8
            if kind == 1:
                o = np.argsort(np.argsort(rng.random((16, S)), axis=0), axis=0)
                z[r, g] = np.where(o < rng.integers(9, 17, S), 255, z[r, g])
            elif kind == 2:
                stage(rng, d, w, r, g)
                few = np.argsort(np.argsort(rng.random((16, 64)), axis=0), axis=0) < np.where(np.arange(64) % 4 == 1, 0, 7)
                d[r, g, :, 16:80] = few * rng.integers(1, 256, (16, 64))
                goal = rng.integers(4, K, S)[:, None]
                v = np.where(kk < goal, rng.integers(16, 80, (S, K)), np.where(kk == goal, W - 1, e[r, g])); v[:, 0] = 0
                m = i % 8 != 5
                e[r, g] = np.where(m[:, None], v, e[r, g]); z[r, g] = np.where(m, 0, z[r, g])
            elif kind == 3 or kind == 6:
                d[r, g] = rng.integers(160, 256, (16, W)); z[r, g] = rng.integers(100, 160, (16, S))
                if kind == 6: d[r, g] = np.where(rng.random(W) < 0.04, rng.integers(0, 100, (16, W)), d[r, g])
            elif kind == 4:
                w[r, g] = 255; half = (rng.permutation(16) < 8)[:, None]
                low = half ^ (rng.random(S) < 0.5)
                z[r, g] = np.where(low, rng.integers(0, 5, (16, S)), rng.integers(251, 256, (16, S)))
                t = rng.random(W); top = np.where(t < 0.3, half, np.where(t < 0.6, ~half, t < 0.85))
                v = np.where(top, rng.integers(251, 256, (16, W)), rng.integers(0, 5, (16, W)))
                d[r, g] = np.where((t >= 0.6) & (t < 0.85), 255, v)
            elif kind == 5:
                e[r, g] = e[r, g, :, :1]
            elif kind == 7:
                w[r, g] = 255; z[r, g] = rng.integers(244, 255, (16, S))
                o = np.argsort(np.argsort(rng.random((16, W)), axis=0), axis=0)
                d[r, g] = np.where((o < rng.integers(8, 17, W)) & (rng.random(W) < 0.6), 255, d[r, g])
    return pack(d, e, z, w)
def setup_inputs_spread(rng):
    d = (np.exp2(8 * rng.random((N, 8, 1, W))) * rng.random((N, 8, 16, W))).astype(np.int64)
    z = (np.exp2(8 * rng.random((N, 8, 1, S))) * rng.random((N, 8, 16, S))).astype(np.int64)
    e = np.minimum((np.exp2((W.bit_length() - 1) * rng.random((N, 8, S, K))) * rng.random((N, 8, S, K))).astype(np.int64), W - 1)
    e = np.where(rng.random((N, 8, S, 1)) < 0.5, W - 1 - e, e)
    w = np.minimum(1 + (np.exp2(8 * rng.random((N, 8, 16))) * rng.random((N, 8, 16))).astype(np.int64), 255)
    return pack(np.minimum(d, 255), e, np.minimum(z, 255), w)
def setup_inputs_ties(rng):
    d, e, z, w = parts(rng)
    d = rng.choice(np.array([0, 0, 100, 252]), (N, 8, 1, W)) + rng.integers(0, 4, d.shape)
    z = rng.choice(np.array([0, 100, 100, 252]), (N, 8, 1, S)) + rng.integers(0, 4, z.shape)
    e[:, :, ::4] = e[:, :, ::4, :1]; e[:, :, 1::4] = rng.choice(np.array([0, 1, W - 2, W - 1]), e[:, :, 1::4].shape)
    e[:, :, 2::4, K // 2:] = e[:, :, 2::4, :K // 2]
    return pack(d, e, z, w)
def check_inputs(d):
    bad = []
    for k, lo, hi in (("dv", 0, 255), ("ef", 0, W - 1), ("zv", 0, 255), ("wt", 1, 255)):
        x = np.asarray(d[k]).astype(np.float32)
        if not np.all((x >= lo) & (x <= hi) & (x == np.floor(x))): bad.append("range of " + k)
    return bad
def reference(dv, ef, zv, wt):
    g2 = np.arange(8)[:, None]; g3 = g2[:, :, None]; kk = np.arange(K - 1)
    D = [np.ascontiguousarray(a.astype(np.float32).astype(np.int32).reshape(8, 16, W).transpose(0, 2, 1)) for a in dv]
    E = [gentries(a).astype(np.int32).reshape(8, S, K) for a in ef]
    z = [np.ascontiguousarray(a.astype(np.float32).astype(np.int32).reshape(8, 16, S).transpose(0, 2, 1)) for a in zv]
    w = wt.astype(np.int32).reshape(N, 8, 1, 1, 16)
    A = [0] * N
    for t in range(RO):
        name = []
        for r in range(N):
            least = 8 + (A[r] & 1); e = E[r]; x = z[r][:, :, None, :]
            n = H(e, U(x, w[r]))
            d = D[r][g3, n]
            a = applies(d, x, least)
            zk = np.where(a[..., None], np.abs(x - d), x); z0 = zk[:, :, :1]
            b = applies(D[r][g3, H(e[:, :, :1], U(zk, w[r]))], zk, least)
            c = applies(D[r][g3, H(e, U(z0, w[r]))], z0, least)
            ok = (b != a[:, :, :1]) & (c == a); ok[:, :, 0] = False
            s = np.argmax(ok, axis=2)
            name.append(np.take_along_axis(n, s[:, :, None], 2)[:, :, 0])
            z[r] = np.take_along_axis(zk, s[:, :, None, None], 2)[:, :, 0]
            E[r] = np.concatenate([np.take_along_axis(e, kk + (kk >= s[:, :, None]), 2), np.zeros((8, S, 1), np.int32)], axis=2)
            A[r] = int(np.count_nonzero(s))
        for r in range(N):
            q = (r - 1 - t % (N - 1)) % N
            E[r][:, :, K - 1] = name[q]
            col = C * np.arange(S) + (name[q] & (C - 1))
            D[r][g2, col] = (D[r][g2, col] + z[q]) >> 1
    return {"yd": np.stack([a.transpose(0, 2, 1).reshape(128, W) for a in D]).astype(np.float32).astype(BF),
            "ye": np.stack([gtable(a.reshape(8, -1)) for a in E]).astype(np.float32),
            "yz": np.stack([a.transpose(0, 2, 1).reshape(128, S) for a in z]).astype(np.float32).astype(BF)}

@@ -1,0 +1,495 @@
+from concourse.mybir import dt, AluOpType, AxisListType, ActivationFunctionType
+
+OP = AluOpType
+AF = ActivationFunctionType
+RO = 4
+SCALE = 4194304.0
+B2, B4, I4, U2 = "bfloat16", "float32", "int32", "uint16"
+SCRATCH = {}
+for _n, _w, _d in (("D", 4096, B2), ("XA0", 4608, B2), ("XA1", 4608, B2), ("XB", 4096, B2), ("GA", 4096, B2), ("GB", 4096, B2),
+                   ("GC", 4096, B2), ("DS", 2048, B2), ("DC", 512, B2), ("FL", 512, I4), ("LN", 256, U2), ("LB", 256, U2),
+                   ("LC", 256, U2), ("LS", 32, U2), ("LD", 32, U2), ("EQ0", 256, B4), ("EQ1", 256, B4), ("VI", 256, I4),
+                   ("VM", 256, I4), ("VF", 256, B4), ("PP", 256, B4), ("SI", 256, I4), ("HI", 256, I4), ("NI", 256, I4),
+                   ("H0", 256, B4), ("T1", 256, B4), ("PQ", 256, B4), ("PK", 256, B4), ("KEY", 256, B4), ("TR", 256, B4),
+                   ("A0T", 32, B4), ("PKS0", 32, I4), ("PKS1", 32, I4), ("TS", 32, I4), ("S0", 32, B2), ("P2", 32, B4),
+                   ("ER", 256, B4), ("MK", 256, B4), ("ME", 256, B4), ("AR", 8, B4), ("AI", 8, I4), ("NM", 32, I4),
+                   ("CI", 32, I4), ("CJ", 32, I4), ("BT", 128, B2), ("BN", 128, B2), ("J8", 32, I4), ("JT", 32, I4),
+                   ("ID", 128, B2), ("NG", 128, B2), ("IDF", 128, B4), ("NGF", 128, B4), ("ON15", 128, B2), ("ONS", 128, B2),
+                   ("OL", 144, B2), ("WL", 144, B2), ("XI", 144, B4), ("CTI", 256, B4), ("PI", 8, I4), ("PJ", 16, I4),
+                   ("PF", 32, B4), ("KM", 16, B4), ("WI", 1, I4), ("WF", 1, B4), ("EFI", 256, I4), ("EF", 256, B4),
+                   ("EH", 256, B2), ("EL", 256, B2), ("YE", 256, B4)):
+    SCRATCH[_n] = ("sbuf", [128, _w], _d)
+for _n in ("bU0", "bU", "bCA", "bCB", "bCC", "bS0", "bS1", "bM"):
+    SCRATCH[_n] = ("psum", [128, 512], B4)
+for _k in range(8):
+    SCRATCH["Q%d" % _k] = ("sbuf", [128, 144], B2)
+    SCRATCH["R%d" % _k] = ("sbuf", [128, 144], B2)
+for _t in range(RO):
+    SCRATCH["LP%d" % _t] = ("sbuf", [128, 32], I4)
+    SCRATCH["LZ%d" % _t] = ("sbuf", [128, 512], B2)
+SEMAPHORES = (["qv", "qs", "qt", "qg"] + ["ldz", "lde", "ldw", "ldd0", "ldd1", "sd0", "sd1", "se", "sz"]
+              + ["%s%d" % (n, t) for t in range(RO) for n in ("an", "az", "ay", "ln", "lz", "ly")])
+
+CFG = {
+    "AS": (1, 6, 3, 7),
+    "CS": (2,),
+    "BS": (2, 7, 6),
+    "NA": "01 23 45 67", "NC": "12 34 56 7", "NB": "12 34 5 67",
+    "V": "gaa5 gaa0 PAR sga5 sga0 gaa2 sga2 gaa4 sga4 HC sgc5 sgc7 sgc1 sgc4 sgc3 sgc6 HB sgb5 sgb3 sgb4 sgb1 PK PQ KEY1 TAIL",
+    "S": "gaa1 gaa6 abs5 abs0 abs6 abs1 sga1 abs2 gaa3 abs4 gaa7 abs3 sga6 sga3 gac2 abs7 sga7 sgc2 H0 gab2 gab7 gab6 sgb2 sgb7 sgb6",
+    "T": "sta1 sta6 U0 U5 na0 U1 na4 sta3 DE U3 sta7 nc7 na2 stc2 U7 na6 nc1 nc5 nc3 nb5 stb2 stb7 nb3 stb6 nb1 nb6",
+}
+
+
+def rank_program(g, core, T, topo):
+    rank = T.rank_of(core)
+    if rank is None:
+        return
+    N = len(T.cores)
+    AS, CS, BS = CFG["AS"], CFG["CS"], CFG["BS"]
+    eng = {"v": g.vector, "s": g.scalar, "t": g.tensor, "g": g, "y": g.sync}
+    qsem = {"v": "qv", "s": "qs", "t": "qt", "g": "qg"}
+    cnt = {"v": 0, "s": 0, "t": 0, "g": 0}
+    known = {q: {} for q in eng}
+    log = {}
+    BANKS = [b for b in SCRATCH if SCRATCH[b][0] == "psum"]
+
+    def need(q, buf, lo, hi, wr):
+        out = []
+        for e in log.get(buf, []):
+            if e[0] < hi and lo < e[1] and (wr or e[2]):
+                out.append(e[4])
+            elif buf in BANKS and e[3] != q:
+                out.append(e[4])
+        return out
+
+    def note(q, buf, lo, hi, wr, op):
+        keep = []
+        for e in log.get(buf, []):
+            covered = lo <= e[0] and e[1] <= hi
+            if covered and (wr or (not e[2] and e[3] == q)):
+                continue
+            keep.append(e)
+        keep.append([lo, hi, wr, q, op])
+        log[buf] = keep
+
+    def settle(q, ops):
+        best = {}
+        for op in ops:
+            if known[q].get(op[0], 0) < op[1]:
+                if op[0] not in best or best[op[0]][1] < op[1]:
+                    best[op[0]] = op
+        for op in sorted(best.values(), key=lambda o: -len(o[2])):
+            if known[q].get(op[0], 0) >= op[1]:
+                continue
+            eng[q].wait_ge(T.sem[op[0]], op[1])
+            for s, v in op[2].items():
+                known[q][s] = max(known[q].get(s, 0), v)
+            known[q][op[0]] = max(known[q].get(op[0], 0), op[1])
+
+    def emit(q, calls, reads, writes, sem=None, val=None, remote=False):
+        ops = []
+        for b, lo, hi in reads:
+            ops += need(q, b, lo, hi, False)
+        for b, lo, hi in writes:
+            ops += need(q, b, lo, hi, True)
+        settle(q, ops)
+        ins = None
+        for c in calls:
+            ins = c(eng[q])
+        snap = dict(known[q])
+        if sem is None:
+            cnt[q] += 1
+            sem, val = qsem[q], cnt[q]
+            ins.then_inc(T.sem[sem], 1)
+        elif not remote:
+            ins.then_inc(T.sem[sem], val)
+        snap[sem] = max(snap.get(sem, 0), val)
+        op = (sem, val, snap)
+        for b, lo, hi in reads:
+            note(q, b, lo, hi, False, op)
+        for b, lo, hi in writes:
+            note(q, b, lo, hi, True, op)
+        return op
+
+    def ap(r):
+        if len(r) > 3:
+            return T[r[0]][:, r[1]:r[2]:r[3]]
+        return T[r[0]][:, r[1]:r[2]]
+
+    def reg(r):
+        return (r[0], r[1], r[2])
+
+    def copy(out, in_):
+        emit("v", [lambda e: e.tensor_copy(ap(out), ap(in_))], [reg(in_)], [reg(out)])
+
+    def tt(out, a, b, op):
+        emit("v", [lambda e: e.tensor_tensor(ap(out), ap(a), ap(b), op)], [reg(a), reg(b)], [reg(out)])
+
+    def ts(out, a, s1, s2, op0, op1=None):
+        rd = [reg(a)] + [reg(s) for s in (s1, s2) if isinstance(s, tuple)]
+        x1 = ap(s1) if isinstance(s1, tuple) else s1
+        x2 = ap(s2) if isinstance(s2, tuple) else s2
+        if op1 is None:
+            emit("v", [lambda e: e.tensor_scalar(ap(out), ap(a), x1, None, op0)], rd, [reg(out)])
+        else:
+            emit("v", [lambda e: e.tensor_scalar(ap(out), ap(a), x1, x2, op0, op1)], rd, [reg(out)])
+
+    def fill(out, c):
+        emit("v", [lambda e: e.memset(ap(out), c)], [], [reg(out)])
+
+    def act(out, in_, func, bias=0.0, scale=1.0):
+        emit("s", [lambda e: e.activation(ap(out), ap(in_), func, bias=bias, scale=scale)], [reg(in_)], [reg(out)])
+
+    def vgather(out, win, off, in1, op):
+        emit("v", [lambda e: e.tensor_tensor(ap(out), ap(win).indirect(ap(off)), ap(in1), op)],
+             [reg(win), reg(off), reg(in1)], [reg(out)])
+
+    def gcopy(q, out, win, off):
+        if q == "v":
+            emit("v", [lambda e: e.tensor_copy(ap(out), ap(win).indirect(ap(off)))], [reg(win), reg(off)], [reg(out)])
+        else:
+            emit("s", [lambda e: e.activation(ap(out), ap(win).indirect(ap(off)), AF.Copy)], [reg(win), reg(off)], [reg(out)])
+
+    def mm(out, parts):
+        n = len(parts)
+        calls = []
+        rd = []
+        for i, (l, r) in enumerate(parts):
+            rd += [reg(l), reg(r)]
+            calls.append(lambda e, l=l, r=r, i=i: e.matmul(ap(out), ap(l), ap(r), i == 0, i == n - 1))
+        emit("t", calls, sorted(set(rd)), [reg(out)])
+
+    def wrapped(out, lbuf, rbuf, lo, hi, extra=()):
+        mm(out, [((lbuf, 15 - r, 143 - r), (rbuf, lo + r, hi, 16)) for r in range(16)] + list(extra))
+
+    def dma(q, out_ap, in_ap, reads, writes, sem):
+        return emit(q, [lambda e: e.dma_start(out=out_ap, in_=in_ap)], reads, writes, sem=sem, val=16)
+
+    def iota(buf, lo, hi, pattern, base, cm, flag):
+        if flag:
+            emit("g", [lambda e: e.iota(T[buf][:, lo:hi], pattern, base, cm, allow_small_or_imprecise_dtypes=True)], [], [(buf, lo, hi)])
+        else:
+            emit("g", [lambda e: e.iota(T[buf][:, lo:hi], pattern, base, cm)], [], [(buf, lo, hi)])
+
+    dma("s", T.EFI[:, :], T.ef[:, :], [], [("EFI", 0, 256)], "lde")
+    dma("y", T.WI[:, :], T.wt[:, :], [], [("WI", 0, 1)], "ldw")
+    dma("y", T.XA0[:, 4096:4608], T.zv[:, :], [], [("XA0", 4096, 4608)], "ldz")
+    dma("y", T.D[:, 0:2048], T.dv[:, 0:2048], [], [("D", 0, 2048)], "ldd0")
+    dma("s", T.D[:, 2048:4096], T.dv[:, 2048:4096], [], [("D", 2048, 4096)], "ldd1")
+
+    iota("PI", 0, 1, [[1, 1]], 0, 1, False)
+    iota("XI", 0, 144, [[1, 144]], 0, 0, True)
+    iota("JT", 0, 32, [[128, 32]], 0, 0, False)
+    iota("CTI", 32, 256, [[-32, 7], [-1, 32]], 287, 0, True)
+    iota("CTI", 0, 32, [[-1, 32]], 31, 0, True)
+    I = ("PI", 0, 1)
+    ts(("PJ", 0, 1), I, 112, None, OP.bitwise_and)
+    ts(("PJ", 1, 2), I, 15, None, OP.bitwise_and)
+    ts(("PJ", 2, 3), I, 3, 1, OP.logical_shift_right, OP.bitwise_and)
+    ts(("PJ", 3, 4), I, 7, None, OP.bitwise_and)
+    ts(("PJ", 4, 5), I, 1, None, OP.bitwise_and)
+    ts(("PJ", 5, 6), I, 1, 7, OP.logical_shift_right, OP.bitwise_and)
+    copy(("PF", 0, 6), ("PJ", 0, 6))
+    copy(("PF", 6, 7), I)
+    tt(("PF", 8, 9), ("PF", 0, 1), ("PF", 2, 3), OP.add)
+    ts(("PF", 9, 10), ("PF", 8, 9), 14.0, None, OP.add)
+    for k in range(8):
+        ts(("KM", k, k + 1), ("PF", 3, 4), float(k), None, OP.is_equal)
+    for k in range(8):
+        ts(("Q%d" % k, 0, 144), ("XI", 0, 144), ("PF", 9, 10), ("KM", k, k + 1), OP.is_equal, OP.mult)
+    copy(("EF", 0, 256), ("EFI", 0, 256))
+    copy(("EH", 0, 256), ("EF", 0, 256))
+    tt(("EL", 0, 256), ("EF", 0, 256), ("EH", 0, 256), OP.subtract)
+    for k in range(8):
+        mm(("bCA" if k < 4 else "bCB", 32 * k, 32 * k + 32),
+           [(("Q%d" % k, 14 - 2 * h, 142 - 2 * h), (e, h, 256, 8)) for h in range(8) for e in ("EH", "EL")])
+    ts(("PF", 10, 11), ("PF", 0, 1), 15.0, None, OP.add)
+    ts(("OL", 0, 144), ("XI", 0, 144), ("PF", 10, 11), SCALE, OP.is_equal, OP.mult)
+    copy(("WF", 0, 1), ("WI", 0, 1))
+    ts(("WL", 0, 144), ("XI", 0, 144), ("PF", 10, 11), ("WF", 0, 1), OP.is_equal, OP.mult)
+    ts(("ID", 0, 128), ("XI", 0, 128), ("PF", 6, 7), None, OP.is_equal)
+    ts(("NG", 0, 128), ("XI", 0, 128), ("PF", 6, 7), -1.0, OP.is_equal, OP.mult)
+    ts(("IDF", 0, 128), ("XI", 0, 128), ("PF", 6, 7), None, OP.is_equal)
+    ts(("NGF", 0, 128), ("XI", 0, 128), ("PF", 6, 7), -1.0, OP.is_equal, OP.mult)
+    fill(("BT", 0, 64), -7.5)
+    fill(("BT", 64, 128), 1.0)
+    fill(("BN", 0, 64), -1.0)
+    fill(("BN", 64, 128), -2.0)
+    fill(("ON15", 0, 128), SCALE / 128)
+    fill(("ONS", 0, 128), 2.0 ** -21)
+    ts(("PF", 11, 12), ("PF", 1, 2), 4592.0, None, OP.add)
+    ts(("PF", 12, 13), ("PF", 1, 2), 8.0, None, OP.mult)
+    ts(("JT", 0, 32), ("JT", 0, 32), 2047, None, OP.bitwise_and)
+    ts(("J8", 0, 32), ("JT", 0, 32), ("PF", 12, 13), None, OP.add)
+    ts(("PF", 13, 14), ("PF", 4, 5), 8.0, 7.0, OP.mult, OP.add)
+    tt(("PF", 14, 15), ("PF", 13, 14), ("PF", 0, 1), OP.add)
+    for h in range(8):
+        ts(("KM", 8 + h, 9 + h), ("PF", 5, 6), float(h), None, OP.is_equal)
+        ts(("R%d" % h, 0, 144), ("XI", 0, 144), ("PF", 14, 15), ("KM", 8 + h, 9 + h), OP.is_equal, OP.mult)
+
+    def second(EQ, lo, hi):
+        act(("bU0", lo, hi), (EQ, lo, hi), AF.Identity, bias=-6722560.0, scale=2080.0)
+
+    def spread_first(EQ):
+        act(("ER", 0, 32), (EQ, 0, 32), AF.Copy)
+        act(("ER", 32, 64), (EQ, 0, 32), AF.Copy)
+        act(("ER", 64, 128), ("ER", 0, 64), AF.Copy)
+        act(("ER", 128, 224), ("ER", 0, 96), AF.Copy)
+        act(("bU0", 256, 480), ("ER", 0, 224), AF.Copy)
+        act(("bU", 288, 512), ("ER", 0, 224), AF.Identity, bias=-6722560.0, scale=2080.0)
+
+    def value(src, lo, hi, dst):
+        n = hi - lo
+        copy(("VI", dst, dst + n), (src, lo, hi))
+        ts(("VM", dst, dst + n), ("VI", dst, dst + n), 4095, None, OP.bitwise_and)
+        ts(("VF", dst, dst + n), ("VM", dst, dst + n), -2048.0, None, OP.add)
+
+    def finish(lo, hi, ni, lst):
+        ts((ni, lo, hi), ("SI", lo, hi), 5, 4095, OP.arith_shift_right, OP.bitwise_and)
+        copy((lst, lo, hi), (ni, lo, hi))
+
+    def hash_many(EQ, k0, k1, ni, lst):
+        for k in range(k0, k1):
+            tt(("PP", 32 * k, 32 * k + 32), (EQ, 32 * k, 32 * k + 32), ("VF", 0, 32), OP.mult)
+        tt(("SI", 32 * k0, 32 * k1), ("PP", 32 * k0, 32 * k1), ("bU0", 32 * k0, 32 * k1), OP.add)
+        finish(32 * k0, 32 * k1, ni, lst)
+
+    def hash_first():
+        tt(("PP", 32, 256), ("bU0", 256, 480), ("VF", 32, 256), OP.mult)
+        tt(("SI", 32, 256), ("PP", 32, 256), ("bU", 288, 512), OP.add)
+        finish(32, 256, "HI", "LB")
+
+    def uz(XA):
+        wrapped(("bU", 256, 288), "WL", XA, 4096, 4608)
+
+    uz("XA0")
+    for h in range(2):
+        b = "bCA" if h == 0 else "bCB"
+        act(("EQ0", 128 * h, 128 * h + 128), (b, 128 * h, 128 * h + 128), AF.Identity, bias=1184.0)
+        second("EQ0", 128 * h, 128 * h + 128)
+    act(("bCC", 256, 512), ("CTI", 0, 256), AF.Copy, scale=4096.0)
+    value("bU", 256, 288, 0)
+    hash_many("EQ0", 0, 4, "NI", "LN")
+    hash_many("EQ0", 4, 8, "NI", "LN")
+    spread_first("EQ0")
+
+    ends = []
+    for t in range(RO):
+        last = t == RO - 1
+        XA, XN = "XA%d" % (t % 2), "XA%d" % ((t + 1) % 2)
+        EQ, EN = "EQ%d" % (t % 2), "EQ%d" % ((t + 1) % 2)
+        PKS = "PKS%d" % (t % 2)
+        ZB = (XA, 4096, 4608)
+        DW = ("D", 0, 4096)
+        tasks = {}
+        order = ["a%d" % k for k in AS] + ["c%d" % k for k in CS] + ["b%d" % k for k in BS]
+
+        def add(name, q, pre, fn):
+            tasks[name] = (q, pre, fn)
+
+        def xa(k):
+            b = (k - 1) % 8
+            return (XA, 512 * b, 512 * b + 512)
+
+        def lst(name, k):
+            return (name, 32 * k, 32 * k + 32)
+
+        def blk(name, k):
+            return (name, 512 * k, 512 * k + 512)
+
+        def bank(name):
+            return ("bS%d" % (order.index(name) % 2), 0, 512)
+
+        def ds(name):
+            i = order.index(name) % 4
+            return ("DS", 512 * i, 512 * i + 512)
+
+        def by_scalar(n, pre, L, k, y, G, extra):
+            i = order.index(n)
+            add("ga" + n, "s", pre, lambda: gcopy("s", ds(n), DW, lst(L, k)))
+            add("st" + n, "t", ["ga" + n] + (["sg" + order[i - 2]] if i >= 2 else []),
+                lambda: mm(bank(n), [(("ID", 0, 128), ds(n)), (("NG", 0, 128), y)]))
+            add("sg" + n, "s", ["st" + n] + extra, lambda: act(blk(G, k), bank(n), AF.Sign, bias=-0.5))
+        for k in range(8):
+            if k in AS:
+                n = "a%d" % k
+                add("abs%d" % k, "s", ["st" + n], lambda n=n, k=k: act(xa(k), bank(n), AF.Abs))
+                by_scalar(n, [], "LN", k, ZB, "GA", ["abs%d" % k])
+            else:
+                add("gaa%d" % k, "v", [], lambda k=k: vgather(blk("XB", k), DW, lst("LN", k), ZB, OP.subtract))
+                add("abs%d" % k, "s", ["gaa%d" % k], lambda k=k: act(xa(k), blk("XB", k), AF.Abs))
+                add("sga%d" % k, "v", ["gaa%d" % k], lambda k=k: ts(blk("GA", k), blk("XB", k), 0.0, None, OP.is_gt))
+            for w, S_, G, L, pre in (("c", CS, "GC", "LC", "HC"), ("b", BS, "GB", "LB", "HB")):
+                if k == 0:
+                    continue
+                n = w + str(k)
+                y = xa(0) if w == "c" else xa(k)
+                if k in S_:
+                    by_scalar(n, [pre], L, k, y, G, [])
+                else:
+                    add("sg" + n, "v", [pre], lambda k=k, G=G, L=L, y=y: vgather(blk(G, k), DW, lst(L, k), y, OP.is_gt))
+
+        def count(w, ks):
+            G, B, S_ = {"a": ("GA", "bCA", AS), "b": ("GB", "bCB", BS), "c": ("GC", "bCC", CS)}[w]
+            kinds = [k in S_ for k in ks]
+            k0, n = ks[0], len(ks)
+            if kinds == sorted(kinds) and n <= 2:
+                b0 = 32 * (2 - n) if not kinds[-1] else 64 - 32 * kinds.count(False)
+                wrapped((B, 32 * k0, 32 * (k0 + n)), "OL", G, 512 * k0, 512 * (k0 + n), [(("ON15", 0, 128), ("BT", b0, b0 + 32 * n))])
+            else:
+                for k in ks:
+                    count(w, [k])
+        for w, c in (("a", "NA"), ("c", "NC"), ("b", "NB")):
+            for grp in CFG[c].split():
+                ks = [int(x) for x in grp]
+                add("n%s%d" % (w, ks[0]), "t", ["sg%s%d" % (w, k) for k in ks] + ["PAR"], lambda w=w, ks=ks: count(w, ks))
+        counts = ["n%s%s" % (w, grp[0]) for w, c in (("a", "NA"), ("c", "NC")) for grp in CFG[c].split()]
+        late = "nb" + CFG["NB"].split()[-1][0]
+        add("U0", "t", ["abs0"], lambda: wrapped(("bM", 288, 320), "WL", XA, 3584, 4096))
+        for ks in ([1, 2], [3, 4], [5, 6], [7]):
+            add("U%d" % ks[0], "t", ["abs%d" % k for k in ks], lambda ks=ks: wrapped(
+                ("bU", 32 * ks[0], 32 * ks[-1] + 32), "WL", XA, 512 * (ks[0] - 1), 512 * ks[-1]))
+
+        def do_par():
+            if t == 0:
+                return
+            emit("v", [lambda e: e.tensor_reduce(T.AR[:, 0:1], T.bM[:, 256:288], AxisListType.X, OP.add)], [("bM", 256, 288)], [("AR", 0, 1)])
+            copy(("AI", 0, 1), ("AR", 0, 1))
+            ts(("AI", 1, 2), ("AI", 0, 1), 1, None, OP.bitwise_and)
+            copy(("AR", 1, 2), ("AI", 1, 2))
+            ts(("BT", 0, 64), ("BN", 0, 64), ("AR", 1, 2), -7.5, OP.mult, OP.add)
+            ts(("BT", 64, 128), ("BN", 64, 128), ("AR", 1, 2), 1.0, OP.mult, OP.add)
+        add("PAR", "v", [], do_par)
+
+        def do_hc():
+            value("bM", 288, 320, 0)
+            hash_many(EQ, 1, 8, "HI", "LC")
+        add("HC", "v", ["U0"], do_hc)
+
+        def do_hb():
+            value("bU", 32, 256, 32)
+            hash_first()
+        add("HB", "v", ["U1", "U3", "U5", "U7", "HC"], do_hb)
+
+        def do_h0():
+            for k in range(1, 8):
+                act(("H0", 32 * k, 32 * k + 32), ("bCA", 0, 32), AF.Copy, scale=-1.0)
+        add("H0", "s", ["na0"], do_h0)
+        add("PK", "v", [], lambda: tt(("PK", 0, 256), ("NI", 0, 256), ("bCC", 256, 512), OP.add))
+
+        def do_pq():
+            ts(("A0T", 0, 32), ("bCA", 0, 32), 0.0, 131072.0, OP.is_gt, OP.mult)
+            tt(("T1", 32, 256), ("bCC", 32, 256), ("H0", 32, 256), OP.max)
+            tt(("KEY", 0, 32), ("PK", 0, 32), ("A0T", 0, 32), OP.add)
+            tt(("bCA", 288, 512), ("bCA", 32, 256), ("T1", 32, 256), OP.min)
+            tt(("PQ", 32, 256), ("PK", 32, 256), ("bCA", 288, 512), OP.min)
+        add("PQ", "v", ["PK", "H0"] + counts, do_pq)
+
+        def key(lo, hi):
+            tt(("bCA", 256 + lo, 256 + hi), ("bCB", lo, hi), ("H0", lo, hi), OP.mult)
+            tt(("KEY", lo, hi), ("PQ", lo, hi), ("bCA", 256 + lo, 256 + hi), OP.min)
+
+        def do_key1():
+            key(32, 192)
+            tt(("TR", 0, 96), ("KEY", 0, 96), ("KEY", 96, 192), OP.max)
+            tt(("TR", 96, 128), ("TR", 0, 32), ("TR", 32, 64), OP.max)
+            tt(("TR", 128, 160), ("TR", 96, 128), ("TR", 64, 96), OP.max)
+        add("KEY1", "v", ["PQ"] + ["nb" + grp[0] for grp in CFG["NB"].split()[:-1]], do_key1)
+
+        def do_tail():
+            key(192, 256)
+            tt(("TR", 160, 192), ("KEY", 192, 224), ("KEY", 224, 256), OP.max)
+            tt((PKS, 0, 32), ("TR", 128, 160), ("TR", 160, 192), OP.max)
+            ts(("TS", 0, 32), (PKS, 0, 32), 12, None, OP.arith_shift_right)
+            ts(("LS", 0, 32), ("TS", 0, 32), -16.0, ("PF", 11, 12), OP.mult, OP.add)
+        add("TAIL", "v", ["KEY1", late], do_tail)
+
+        def do_de():
+            mm(("bM", 0, 224), [(("IDF", 0, 128), (EQ, 32, 256)), (("NGF", 0, 128), (EQ, 0, 224))])
+        add("DE", "t", ["HC", "PAR"], do_de)
+
+        lists = {"v": CFG["V"].split(), "s": CFG["S"].split(), "t": CFG["T"].split()}
+        assert sorted(lists["v"] + lists["s"] + lists["t"]) == sorted(tasks), set(tasks) ^ set(lists["v"] + lists["s"] + lists["t"])
+        done = set()
+        pos = {"v": 0, "s": 0, "t": 0}
+        while len(done) < len(tasks):
+            moved = False
+            for q in ("v", "s", "t"):
+                while pos[q] < len(lists[q]) and all(p in done for p in tasks[lists[q][pos[q]]][1]):
+                    nm = lists[q][pos[q]]
+                    assert tasks[nm][0] == q
+                    tasks[nm][2]()
+                    done.add(nm)
+                    pos[q] += 1
+                    moved = True
+            assert moved, [lists[q][pos[q]:pos[q] + 1] for q in lists]
+
+        dst = T.cores[(rank + 1 + t % (N - 1)) % N]
+        rid, pid = topo.addr(dst)[0], topo.addr(dst)[1]
+        mask = topo.mask(core, dst)
+        ne = len(topo.engines(core, dst))
+
+        def send(out, in_, rsem, lsem):
+            return emit("g", [lambda e: e.remote_dma(ap(out), ap(in_), T.sem[rsem], T.sem[lsem], pid, rid, mask)],
+                        [reg(in_)], [], sem=lsem, val=ne, remote=True)
+
+        def landed(buf, lo, hi, rsem):
+            note("g", buf, lo, hi, True, (rsem, ne, {rsem: ne}))
+        LP, LZ = "LP%d" % t, "LZ%d" % t
+        ends.append(send((LP, 0, 32), (PKS, 0, 32), "an%d" % t, "ln%d" % t))
+        gcopy("v", (XN, 4096, 4352), (XA, 0, 4608), ("LS", 0, 16))
+        gcopy("s", (XN, 4352, 4608), (XA, 0, 4608), ("LS", 16, 32))
+        ends.append(send((LZ, 0, 256), (XN, 4096, 4352), "az%d" % t, "lz%d" % t))
+        ends.append(send((LZ, 256, 512), (XN, 4352, 4608), "ay%d" % t, "ly%d" % t))
+        landed(LP, 0, 32, "an%d" % t)
+        landed(LZ, 0, 256, "az%d" % t)
+        landed(LZ, 256, 512, "ay%d" % t)
+
+        ts(("S0", 0, 32), (PKS, 0, 32), 262144.0, 2097152.0, OP.is_lt, OP.mult)
+        tt(("P2", 0, 32), (PKS, 0, 32), ("S0", 0, 32), OP.add)
+        for k in range(7):
+            act(("MK", 32 * k, 32 * k + 32), ("P2", 0, 32), AF.Sign, bias=0.5 - (9 - k) * 131072)
+        act(("ME", 0, 224), ("MK", 0, 224), AF.Relu)
+        if not last:
+            uz(XN)
+            mm(("bM", 256, 288), [(("ONS", 0, 128), ("S0", 0, 32))])
+            value("bU", 256, 288, 0)
+        tt(("bM", 0, 224), ("bM", 0, 224), ("ME", 0, 224), OP.mult)
+        tt((EN, 0, 224), ("bM", 0, 224), (EQ, 0, 224), OP.add)
+        if not last:
+            second(EN, 0, 224)
+        ts(("CI", 0, 32), (LP, 0, 32), 7, None, OP.bitwise_and)
+        tt(("CJ", 0, 32), ("CI", 0, 32), ("J8", 0, 32), OP.add)
+        copy(("LD", 0, 32), ("CJ", 0, 32))
+        ts(("NM", 0, 32), (LP, 0, 32), 4095, None, OP.bitwise_and)
+        ts((EN, 224, 256), ("NM", 0, 32), 1184.0, None, OP.add)
+        for h in range(2):
+            gcopy("s", ("DC", 256 * h, 256 * h + 256), ("D", 2048 * h, 2048 * h + 2048), ("LD", 16 * h, 16 * h + 16))
+        if not last:
+            second(EN, 224, 256)
+            hash_many(EN, 0, 8, "NI", "LN")
+        else:
+            copy(("EH", 0, 256), (EN, 0, 256))
+            tt(("EL", 0, 256), (EN, 0, 256), ("EH", 0, 256), OP.subtract)
+        for h in range(2):
+            R = (256 * h, 256 * h + 256)
+            mm(("bS%d" % h, 0, 256), [(("ID", 0, 128), ("DC",) + R), (("ID", 0, 128), (LZ,) + R)])
+        for h in range(2):
+            R = (256 * h, 256 * h + 256)
+            ts(("FL",) + R, ("bS%d" % h, 0, 256), 0.5, -0.25, OP.mult, OP.add)
+            emit("v", [lambda e, h=h, R=R: e.tensor_copy(T.D[:, 2048 * h:2048 * h + 2048].indirect(T.LD[:, 16 * h:16 * h + 16]), T.FL[:, R[0]:R[1]])],
+                 [("FL",) + R, ("LD", 16 * h, 16 * h + 16)], [("D", 2048 * h, 2048 * h + 2048)])
+            if last:
+                ends.append(dma("y", T.yd[:, 2048 * h:2048 * h + 2048], T.D[:, 2048 * h:2048 * h + 2048],
+                                [("D", 2048 * h, 2048 * h + 2048)], [], "sd%d" % h))
+        if not last:
+            spread_first(EN)
+        else:
+            for h in range(8):
+                mm(("bM", 256 + h, 512, 8), [(("R%d" % h, 7 - k, 135 - k), (e, 32 * k, 32 * k + 32)) for k in range(8) for e in ("EH", "EL")])
+            act(("YE", 0, 256), ("bM", 256, 512), AF.Identity, bias=-1184.0)
+            ends.append(dma("s", T.yz[:, :], T[XN][:, 4096:4608], [(XN, 4096, 4608)], [], "sz"))
+            ends.append(dma("s", T.ye[:, :], T.YE[:, :], [("YE", 0, 256)], [], "se"))
+    settle("g", ends)
+    settle("g", [(qsem[q], cnt[q], {}) for q in "vstg"])

@@ -3,21 +3,24 @@ from concourse.mybir import dt, AluOpType, AxisListType, ActivationFunctionType
 OP = AluOpType
 AF = ActivationFunctionType
 RO = 4
+BIG = 1.5 * 2.0 ** 35
+MID = 1.5 * 2.0 ** 23
 SCALE = 4194304.0
 B2, B4, I4, U2 = "bfloat16", "float32", "int32", "uint16"
 SCRATCH = {}
 for _n, _w, _d in (("D", 4096, B2), ("XA0", 4608, B2), ("XA1", 4608, B2), ("XB", 4096, B2), ("GA", 4096, B2), ("GB", 4096, B2),
                    ("GC", 4096, B2), ("DS", 2048, B2), ("DC", 512, B2), ("FL", 512, I4), ("LN", 256, U2), ("LB", 256, U2),
-                   ("LC", 256, U2), ("LS", 32, U2), ("LD", 32, U2), ("EQ0", 256, B4), ("EQ1", 256, B4), ("VI", 256, I4),
-                   ("VM", 256, I4), ("VF", 256, B4), ("PP", 256, B4), ("SI", 256, I4), ("HI", 256, I4), ("NI", 256, I4),
+                   ("LC", 256, U2), ("LS", 32, U2), ("LD", 32, U2), ("EQ0", 256, B4), ("EQ1", 256, B4), ("VF", 256, B4), ("PP", 256, B4), ("SI", 256, I4), ("HI", 256, I4), ("NI", 256, I4),
                    ("H0", 256, B4), ("T1", 256, B4), ("PQ", 256, B4), ("PK", 256, B4), ("KEY", 256, B4), ("TR", 256, B4),
                    ("A0T", 32, B4), ("PKS0", 32, I4), ("PKS1", 32, I4), ("TS", 32, I4), ("S0", 32, B2), ("P2", 32, B4),
-                   ("ER", 256, B4), ("MK", 256, B4), ("ME", 256, B4), ("AR", 8, B4), ("AI", 8, I4), ("NM", 32, I4),
-                   ("CI", 32, I4), ("CJ", 32, I4), ("BT", 128, B2), ("BN", 128, B2), ("J8", 32, I4), ("JT", 32, I4),
+                   ("ER", 256, B4), ("MK", 256, B4), ("AR", 8, B4), ("AJ", 32, B4), ("NM", 32, I4),
+                   ("CI", 32, I4), ("CJ", 32, I4), ("BT", 192, B2), ("BN", 192, B2), ("J8", 32, I4), ("JT", 32, I4),
                    ("ID", 128, B2), ("NG", 128, B2), ("IDF", 128, B4), ("NGF", 128, B4), ("ON15", 128, B2), ("ONS", 128, B2),
                    ("OL", 144, B2), ("WL", 144, B2), ("XI", 144, B4), ("CTI", 256, B4), ("PI", 8, I4), ("PJ", 16, I4),
                    ("PF", 32, B4), ("KM", 16, B4), ("WI", 1, I4), ("WF", 1, B4), ("EFI", 256, I4), ("EF", 256, B4),
-                   ("EH", 256, B2), ("EL", 256, B2), ("YE", 256, B4)):
+                   ("EH", 256, B2), ("EL", 256, B2), ("EHL", 512, B2), ("J4", 32, I4), ("JU", 32, I4), ("K2", 96, B2),
+                   ("K3", 256, B2), ("RX", 256, B4), ("RR", 256, B4), ("HP", 256, B2), ("BI", 128, B2), ("FX", 256, B4),
+                   ("FB", 256, B2), ("YE", 256, B4)):
     SCRATCH[_n] = ("sbuf", [128, _w], _d)
 for _n in ("bU0", "bU", "bCA", "bCB", "bCC", "bS0", "bS1", "bM"):
     SCRATCH[_n] = ("psum", [128, 512], B4)
@@ -27,17 +30,19 @@ for _k in range(8):
 for _t in range(RO):
     SCRATCH["LP%d" % _t] = ("sbuf", [128, 32], I4)
     SCRATCH["LZ%d" % _t] = ("sbuf", [128, 512], B2)
-SEMAPHORES = (["qv", "qs", "qt", "qg"] + ["ldz", "lde", "ldw", "ldd0", "ldd1", "sd0", "sd1", "se", "sz"]
+SEMAPHORES = (["qv", "qs", "qt", "qg"] + ["ldz", "lde", "ldw", "ldd0", "ldd1", "sd0", "sd1", "sd2", "sd3", "se", "sz"]
               + ["%s%d" % (n, t) for t in range(RO) for n in ("an", "az", "ay", "ln", "lz", "ly")])
 
 CFG = {
-    "AS": (1, 6, 3, 7),
-    "CS": (2,),
-    "BS": (2, 7, 6),
-    "NA": "01 23 45 67", "NC": "12 34 56 7", "NB": "12 34 5 67",
-    "V": "gaa5 gaa0 PAR sga5 sga0 gaa2 sga2 gaa4 sga4 HC sgc5 sgc7 sgc1 sgc4 sgc3 sgc6 HB sgb5 sgb3 sgb4 sgb1 PK PQ KEY1 TAIL",
-    "S": "gaa1 gaa6 abs5 abs0 abs6 abs1 sga1 abs2 gaa3 abs4 gaa7 abs3 sga6 sga3 gac2 abs7 sga7 sgc2 H0 gab2 gab7 gab6 sgb2 sgb7 sgb6",
-    "T": "sta1 sta6 U0 U5 na0 U1 na4 sta3 DE U3 sta7 nc7 na2 stc2 U7 na6 nc1 nc5 nc3 nb5 stb2 stb7 nb3 stb6 nb1 nb6",
+    "AS": (7, 1, 5),
+    "CS": (4, 5),
+    "BS": (3, 5),
+    "NA": "01 23 45 67", "NC": "123 45 67", "NB": "123 45 67",
+    "NU": "12 34 56 7",
+    "BM": (1, 6),
+    "V": "gaa0 gaa6 gaa3 gaa2 gaa4 sga2 sga6 sga0 sga3 HC sga4 sgc3 sgc6 sgc2 sgc1 sgc7 HB sgb1 sgb2 sgb4 PQ sgb6 sgb7 KEY1 TAIL",
+    "S": "gaa7 gaa1 abs7 abs0 sga7 gaa5 abs2 RC abs4 abs1 sga1 abs3 abs6 gac4 abs5 H0 RB sgc4 sga5 gac5 gab3 sgc5 gab5 sgb3 sgb5",
+    "T": "sta7 sta1 U7 U0 na6 na2 U1 sta5 na0 U3 stc4 U5 nc1 nc6 na4 stc5 stb3 nc4 stb5 nb1 nb4 nb6",
 }
 
 
@@ -139,7 +144,10 @@ def rank_program(g, core, T, topo):
         emit("v", [lambda e: e.memset(ap(out), c)], [], [reg(out)])
 
     def act(out, in_, func, bias=0.0, scale=1.0):
-        emit("s", [lambda e: e.activation(ap(out), ap(in_), func, bias=bias, scale=scale)], [reg(in_)], [reg(out)])
+        rd = [reg(x) for x in (in_, bias, scale) if isinstance(x, tuple)]
+        b = ap(bias) if isinstance(bias, tuple) else bias
+        k = ap(scale) if isinstance(scale, tuple) else scale
+        emit("s", [lambda e: e.activation(ap(out), ap(in_), func, bias=b, scale=k)], rd, [reg(out)])
 
     def vgather(out, win, off, in1, op):
         emit("v", [lambda e: e.tensor_tensor(ap(out), ap(win).indirect(ap(off)), ap(in1), op)],
@@ -199,11 +207,18 @@ def rank_program(g, core, T, topo):
     for k in range(8):
         ts(("Q%d" % k, 0, 144), ("XI", 0, 144), ("PF", 9, 10), ("KM", k, k + 1), OP.is_equal, OP.mult)
     copy(("EF", 0, 256), ("EFI", 0, 256))
-    copy(("EH", 0, 256), ("EF", 0, 256))
-    tt(("EL", 0, 256), ("EF", 0, 256), ("EH", 0, 256), OP.subtract)
-    for k in range(8):
-        mm(("bCA" if k < 4 else "bCB", 32 * k, 32 * k + 32),
-           [(("Q%d" % k, 14 - 2 * h, 142 - 2 * h), (e, h, 256, 8)) for h in range(8) for e in ("EH", "EL")])
+
+    def split(E, lo, hi, step):
+        a = ("EH", lo, hi) if step == 1 else ("EHL", 2 * lo, 2 * hi, 2)
+        b = ("EL", lo, hi) if step == 1 else ("EHL", 2 * lo + 1, 2 * hi, 2)
+        copy(a, (E, lo, hi))
+        tt(b, (E, lo, hi), a, OP.subtract)
+    split("EF", 0, 256, 1)
+
+    def bring(b, k):
+        mm((b, 32 * k, 32 * k + 32), [(("Q%d" % k, 14 - 2 * h, 142 - 2 * h), (e, h, 256, 8)) for h in range(8) for e in ("EH", "EL")])
+    for k in range(4):
+        bring("bCA", k)
     ts(("PF", 10, 11), ("PF", 0, 1), 15.0, None, OP.add)
     ts(("OL", 0, 144), ("XI", 0, 144), ("PF", 10, 11), SCALE, OP.is_equal, OP.mult)
     copy(("WF", 0, 1), ("WI", 0, 1))
@@ -212,16 +227,20 @@ def rank_program(g, core, T, topo):
     ts(("NG", 0, 128), ("XI", 0, 128), ("PF", 6, 7), -1.0, OP.is_equal, OP.mult)
     ts(("IDF", 0, 128), ("XI", 0, 128), ("PF", 6, 7), None, OP.is_equal)
     ts(("NGF", 0, 128), ("XI", 0, 128), ("PF", 6, 7), -1.0, OP.is_equal, OP.mult)
-    fill(("BT", 0, 64), -7.5)
-    fill(("BT", 64, 128), 1.0)
-    fill(("BN", 0, 64), -1.0)
-    fill(("BN", 64, 128), -2.0)
+    fill(("BT", 0, 96), -7.5)
+    fill(("BT", 96, 192), 1.0)
+    fill(("BN", 0, 96), -1.0)
+    fill(("BN", 96, 192), -2.0)
     fill(("ON15", 0, 128), SCALE / 128)
+    fill(("K2", 0, 96), 2048 / SCALE)
+    fill(("K3", 0, 256), -0.5 / SCALE)
+    ts(("BI", 0, 128), ("XI", 0, 128), ("PF", 6, 7), 64 * SCALE, OP.is_equal, OP.mult)
     fill(("ONS", 0, 128), 2.0 ** -21)
     ts(("PF", 11, 12), ("PF", 1, 2), 4592.0, None, OP.add)
     ts(("PF", 12, 13), ("PF", 1, 2), 8.0, None, OP.mult)
-    ts(("JT", 0, 32), ("JT", 0, 32), 2047, None, OP.bitwise_and)
-    ts(("J8", 0, 32), ("JT", 0, 32), ("PF", 12, 13), None, OP.add)
+    for j, m in (("J8", 2047), ("J4", 1023)):
+        ts(("JU", 0, 32), ("JT", 0, 32), m, None, OP.bitwise_and)
+        ts((j, 0, 32), ("JU", 0, 32), ("PF", 12, 13), None, OP.add)
     ts(("PF", 13, 14), ("PF", 4, 5), 8.0, 7.0, OP.mult, OP.add)
     tt(("PF", 14, 15), ("PF", 13, 14), ("PF", 0, 1), OP.add)
     for h in range(8):
@@ -239,19 +258,28 @@ def rank_program(g, core, T, topo):
         act(("bU0", 256, 480), ("ER", 0, 224), AF.Copy)
         act(("bU", 288, 512), ("ER", 0, 224), AF.Identity, bias=-6722560.0, scale=2080.0)
 
-    def value(src, lo, hi, dst):
-        n = hi - lo
-        copy(("VI", dst, dst + n), (src, lo, hi))
-        ts(("VM", dst, dst + n), ("VI", dst, dst + n), 4095, None, OP.bitwise_and)
-        ts(("VF", dst, dst + n), ("VM", dst, dst + n), -2048.0, None, OP.add)
+    def round_s(src, lo):
+        n = src[2] - src[1]
+        act(("RX", lo, lo + n), src, AF.Identity, bias=BIG, scale=1.0 + 2.0 ** -22)
+        act(("RR", lo, lo + n), ("RX", lo, lo + n), AF.Identity, bias=-BIG)
+
+    def value_v(src, lo):
+        n = src[2] - src[1]
+        tt(("VF", lo, lo + n), src, ("RR", lo, lo + n), OP.subtract)
 
     def finish(lo, hi, ni, lst):
         ts((ni, lo, hi), ("SI", lo, hi), 5, 4095, OP.arith_shift_right, OP.bitwise_and)
         copy((lst, lo, hi), (ni, lo, hi))
 
     def hash_many(EQ, k0, k1, ni, lst):
+        products(EQ, k0, k1)
+        names(k0, k1, ni, lst)
+
+    def products(EQ, k0, k1):
         for k in range(k0, k1):
             tt(("PP", 32 * k, 32 * k + 32), (EQ, 32 * k, 32 * k + 32), ("VF", 0, 32), OP.mult)
+
+    def names(k0, k1, ni, lst):
         tt(("SI", 32 * k0, 32 * k1), ("PP", 32 * k0, 32 * k1), ("bU0", 32 * k0, 32 * k1), OP.add)
         finish(32 * k0, 32 * k1, ni, lst)
 
@@ -261,18 +289,24 @@ def rank_program(g, core, T, topo):
         finish(32, 256, "HI", "LB")
 
     def uz(XA):
-        wrapped(("bU", 256, 288), "WL", XA, 4096, 4608)
+        wrapped(("bU", 256, 288), "WL", XA, 4096, 4608, [(("ON15", 0, 128), ("K2", 0, 32))])
 
     uz("XA0")
-    for h in range(2):
-        b = "bCA" if h == 0 else "bCB"
+    for k in range(4, 8):
+        bring("bCB", k)
+    act(("bCC", 256, 512), ("CTI", 0, 256), AF.Copy, scale=4096.0)
+    for h, b in ((0, "bCA"), (1, "bCB")):
         act(("EQ0", 128 * h, 128 * h + 128), (b, 128 * h, 128 * h + 128), AF.Identity, bias=1184.0)
         second("EQ0", 128 * h, 128 * h + 128)
-    act(("bCC", 256, 512), ("CTI", 0, 256), AF.Copy, scale=4096.0)
-    value("bU", 256, 288, 0)
-    hash_many("EQ0", 0, 4, "NI", "LN")
-    hash_many("EQ0", 4, 8, "NI", "LN")
+        if h == 0:
+            round_s(("bU", 256, 288), 0)
+            value_v(("bU", 256, 288), 0)
+        hash_many("EQ0", 4 * h, 4 * h + 4, "NI", "LN")
     spread_first("EQ0")
+
+    def packs():
+        tt(("PK", 0, 256), ("NI", 0, 256), ("bCC", 256, 512), OP.add)
+    packs()
 
     ends = []
     for t in range(RO):
@@ -327,6 +361,11 @@ def rank_program(g, core, T, topo):
                 y = xa(0) if w == "c" else xa(k)
                 if k in S_:
                     by_scalar(n, [pre], L, k, y, G, [])
+                elif w == "b" and k in CFG["BM"]:
+                    add("sg" + n, "v", [pre], lambda k=k: vgather(("GB", 512 * k, 512 * k + 1024), DW, ("LB", 32 * k, 32 * k + 64),
+                                                                  (XA, 512 * k - 512, 512 * k + 512), OP.is_gt))
+                elif w == "b" and k - 1 in CFG["BM"]:
+                    add("sg" + n, "v", ["sgb%d" % (k - 1)], lambda: None)
                 else:
                     add("sg" + n, "v", [pre], lambda k=k, G=G, L=L, y=y: vgather(blk(G, k), DW, lst(L, k), y, OP.is_gt))
 
@@ -334,60 +373,71 @@ def rank_program(g, core, T, topo):
             G, B, S_ = {"a": ("GA", "bCA", AS), "b": ("GB", "bCB", BS), "c": ("GC", "bCC", CS)}[w]
             kinds = [k in S_ for k in ks]
             k0, n = ks[0], len(ks)
-            if kinds == sorted(kinds) and n <= 2:
-                b0 = 32 * (2 - n) if not kinds[-1] else 64 - 32 * kinds.count(False)
-                wrapped((B, 32 * k0, 32 * (k0 + n)), "OL", G, 512 * k0, 512 * (k0 + n), [(("ON15", 0, 128), ("BT", b0, b0 + 32 * n))])
+            if kinds == sorted(kinds):
+                b0 = 96 - 32 * kinds.count(False)
+                o = 32 * k0
+                if w == "b" and k0 >= 6:
+                    B, o = "bM", 32 * k0 + 128
+                extra = [(("ON15", 0, 128), ("BT", b0, b0 + 32 * n))]
+                if w == "c":
+                    extra.append((("BI", 0, 128), ("HP", 32 * k0, 32 * (k0 + n))))
+                wrapped((B, o, o + 32 * n), "OL", G, 512 * k0, 512 * (k0 + n), extra)
             else:
                 for k in ks:
                     count(w, [k])
         for w, c in (("a", "NA"), ("c", "NC"), ("b", "NB")):
             for grp in CFG[c].split():
                 ks = [int(x) for x in grp]
-                add("n%s%d" % (w, ks[0]), "t", ["sg%s%d" % (w, k) for k in ks] + ["PAR"], lambda w=w, ks=ks: count(w, ks))
+                add("n%s%d" % (w, ks[0]), "t", ["sg%s%d" % (w, k) for k in ks] + (["H0"] if w == "c" else []), lambda w=w, ks=ks: count(w, ks))
         counts = ["n%s%s" % (w, grp[0]) for w, c in (("a", "NA"), ("c", "NC")) for grp in CFG[c].split()]
         late = "nb" + CFG["NB"].split()[-1][0]
-        add("U0", "t", ["abs0"], lambda: wrapped(("bM", 288, 320), "WL", XA, 3584, 4096))
-        for ks in ([1, 2], [3, 4], [5, 6], [7]):
+        add("U0", "t", ["abs0"], lambda: wrapped(("bM", 288, 320), "WL", XA, 3584, 4096, [(("ON15", 0, 128), ("K2", 0, 32))]))
+        add("RC", "s", ["U0"], lambda: round_s(("bM", 288, 320), 0))
+        UG = [[int(x) for x in grp] for grp in CFG["NU"].split()]
+        for ks in UG:
             add("U%d" % ks[0], "t", ["abs%d" % k for k in ks], lambda ks=ks: wrapped(
-                ("bU", 32 * ks[0], 32 * ks[-1] + 32), "WL", XA, 512 * (ks[0] - 1), 512 * ks[-1]))
+                ("bU", 32 * ks[0], 32 * ks[-1] + 32), "WL", XA, 512 * (ks[0] - 1), 512 * ks[-1],
+                [(("ON15", 0, 128), ("K2", 0, 32 * len(ks)))]))
 
         def do_par():
-            if t == 0:
-                return
-            emit("v", [lambda e: e.tensor_reduce(T.AR[:, 0:1], T.bM[:, 256:288], AxisListType.X, OP.add)], [("bM", 256, 288)], [("AR", 0, 1)])
-            copy(("AI", 0, 1), ("AR", 0, 1))
-            ts(("AI", 1, 2), ("AI", 0, 1), 1, None, OP.bitwise_and)
-            copy(("AR", 1, 2), ("AI", 1, 2))
-            ts(("BT", 0, 64), ("BN", 0, 64), ("AR", 1, 2), -7.5, OP.mult, OP.add)
-            ts(("BT", 64, 128), ("BN", 64, 128), ("AR", 1, 2), 1.0, OP.mult, OP.add)
-        add("PAR", "v", [], do_par)
+            emit("s", [lambda e: e.activation(T.AJ[:, 0:32], T.bM[:, 256:288], AF.Copy, accum_out=T.AR[:, 0:1])],
+                 [("bM", 256, 288)], [("AJ", 0, 32), ("AR", 0, 1)])
+            act(("AR", 1, 2), ("AR", 0, 1), AF.Identity, bias=MID, scale=0.5)
+            act(("AR", 2, 3), ("AR", 1, 2), AF.Identity, bias=2 * MID, scale=-2.0)
+            act(("AR", 3, 4), ("AR", 2, 3), AF.Abs, bias=("AR", 0, 1))
+            for lo, b in ((0, -7.5), (96, 1.0)):
+                act(("BT", lo, lo + 96), ("BN", lo, lo + 96), AF.Identity, bias=b, scale=("AR", 3, 4))
 
         def do_hc():
-            value("bM", 288, 320, 0)
+            value_v(("bM", 288, 320), 0)
             hash_many(EQ, 1, 8, "HI", "LC")
-        add("HC", "v", ["U0"], do_hc)
+        add("HC", "v", ["RC"], do_hc)
+
+        def do_rb():
+            round_s(("bU", 32, 256), 32)
+        add("RB", "s", ["U%d" % ks[0] for ks in UG], do_rb)
 
         def do_hb():
-            value("bU", 32, 256, 32)
+            value_v(("bU", 32, 256), 32)
             hash_first()
-        add("HB", "v", ["U1", "U3", "U5", "U7", "HC"], do_hb)
+        add("HB", "v", ["RB", "HC"], do_hb)
 
         def do_h0():
             for k in range(1, 8):
                 act(("H0", 32 * k, 32 * k + 32), ("bCA", 0, 32), AF.Copy, scale=-1.0)
+            act(("HP", 32, 256), ("H0", 32, 256), AF.Relu, scale=1.0 / SCALE)
         add("H0", "s", ["na0"], do_h0)
-        add("PK", "v", [], lambda: tt(("PK", 0, 256), ("NI", 0, 256), ("bCC", 256, 512), OP.add))
 
         def do_pq():
             ts(("A0T", 0, 32), ("bCA", 0, 32), 0.0, 131072.0, OP.is_gt, OP.mult)
-            tt(("T1", 32, 256), ("bCC", 32, 256), ("H0", 32, 256), OP.max)
+            tt(("T1", 32, 256), ("bCC", 32, 256), ("PK", 32, 256), OP.min)
             tt(("KEY", 0, 32), ("PK", 0, 32), ("A0T", 0, 32), OP.add)
-            tt(("bCA", 288, 512), ("bCA", 32, 256), ("T1", 32, 256), OP.min)
-            tt(("PQ", 32, 256), ("PK", 32, 256), ("bCA", 288, 512), OP.min)
-        add("PQ", "v", ["PK", "H0"] + counts, do_pq)
+            tt(("PQ", 32, 256), ("bCA", 32, 256), ("T1", 32, 256), OP.min)
+        add("PQ", "v", ["H0"] + counts, do_pq)
 
         def key(lo, hi):
-            tt(("bCA", 256 + lo, 256 + hi), ("bCB", lo, hi), ("H0", lo, hi), OP.mult)
+            cb = ("bCB", lo, hi) if lo < 192 else ("bM", lo + 128, hi + 128)
+            tt(("bCA", 256 + lo, 256 + hi), cb, ("H0", lo, hi), OP.mult)
             tt(("KEY", lo, hi), ("PQ", lo, hi), ("bCA", 256 + lo, 256 + hi), OP.min)
 
         def do_key1():
@@ -405,10 +455,6 @@ def rank_program(g, core, T, topo):
             ts(("LS", 0, 32), ("TS", 0, 32), -16.0, ("PF", 11, 12), OP.mult, OP.add)
         add("TAIL", "v", ["KEY1", late], do_tail)
 
-        def do_de():
-            mm(("bM", 0, 224), [(("IDF", 0, 128), (EQ, 32, 256)), (("NGF", 0, 128), (EQ, 0, 224))])
-        add("DE", "t", ["HC", "PAR"], do_de)
-
         lists = {"v": CFG["V"].split(), "s": CFG["S"].split(), "t": CFG["T"].split()}
         assert sorted(lists["v"] + lists["s"] + lists["t"]) == sorted(tasks), set(tasks) ^ set(lists["v"] + lists["s"] + lists["t"])
         done = set()
@@ -424,6 +470,8 @@ def rank_program(g, core, T, topo):
                     pos[q] += 1
                     moved = True
             assert moved, [lists[q][pos[q]:pos[q] + 1] for q in lists]
+
+        mm(("bCB", 256, 480), [(("IDF", 0, 128), (EQ, 32, 256)), (("NGF", 0, 128), (EQ, 0, 224))])
 
         dst = T.cores[(rank + 1 + t % (N - 1)) % N]
         rid, pid = topo.addr(dst)[0], topo.addr(dst)[1]
@@ -448,47 +496,66 @@ def rank_program(g, core, T, topo):
 
         ts(("S0", 0, 32), (PKS, 0, 32), 262144.0, 2097152.0, OP.is_lt, OP.mult)
         tt(("P2", 0, 32), (PKS, 0, 32), ("S0", 0, 32), OP.add)
+        if not last:
+            mm(("bM", 256, 288), [(("ONS", 0, 128), ("S0", 0, 32))])
         for k in range(7):
-            act(("MK", 32 * k, 32 * k + 32), ("P2", 0, 32), AF.Sign, bias=0.5 - (9 - k) * 131072)
-        act(("ME", 0, 224), ("MK", 0, 224), AF.Relu)
+            ts(("MK", 32 * k, 32 * k + 32), ("P2", 0, 32), float((9 - k) * 131072), None, OP.is_ge)
         if not last:
             uz(XN)
-            mm(("bM", 256, 288), [(("ONS", 0, 128), ("S0", 0, 32))])
-            value("bU", 256, 288, 0)
-        tt(("bM", 0, 224), ("bM", 0, 224), ("ME", 0, 224), OP.mult)
-        tt((EN, 0, 224), ("bM", 0, 224), (EQ, 0, 224), OP.add)
+            round_s(("bU", 256, 288), 0)
+        tt(("bCB", 256, 480), ("bCB", 256, 480), ("MK", 0, 224), OP.mult)
+        tt((EN, 0, 224), ("bCB", 256, 480), (EQ, 0, 224), OP.add)
         if not last:
             second(EN, 0, 224)
-        ts(("CI", 0, 32), (LP, 0, 32), 7, None, OP.bitwise_and)
-        tt(("CJ", 0, 32), ("CI", 0, 32), ("J8", 0, 32), OP.add)
-        copy(("LD", 0, 32), ("CJ", 0, 32))
+            value_v(("bU", 256, 288), 0)
+            do_par()
+            products(EN, 0, 7)
+        else:
+            split(EN, 0, 224, 2)
+        J, nq = ("J4", 4) if last else ("J8", 2)
         ts(("NM", 0, 32), (LP, 0, 32), 4095, None, OP.bitwise_and)
+        ts(("CI", 0, 32), (LP, 0, 32), 7, None, OP.bitwise_and)
         ts((EN, 224, 256), ("NM", 0, 32), 1184.0, None, OP.add)
-        for h in range(2):
-            gcopy("s", ("DC", 256 * h, 256 * h + 256), ("D", 2048 * h, 2048 * h + 2048), ("LD", 16 * h, 16 * h + 16))
+        tt(("CJ", 0, 32), ("CI", 0, 32), (J, 0, 32), OP.add)
+        copy(("LD", 0, 32), ("CJ", 0, 32))
         if not last:
             second(EN, 224, 256)
-            hash_many(EN, 0, 8, "NI", "LN")
+        WQ, SQ, CQ = 4096 // nq, 512 // nq, 32 // nq
+        parts = [((SQ * q, SQ * q + SQ), (WQ * q, WQ * q + WQ), (CQ * q, CQ * q + CQ)) for q in range(nq)]
+        for q, (R, W, C) in enumerate(parts):
+            gcopy("s", ("DC",) + R, ("D",) + W, ("LD",) + C)
+        if not last:
+            products(EN, 7, 8)
+            names(0, 8, "NI", "LN")
+            packs()
         else:
-            copy(("EH", 0, 256), (EN, 0, 256))
-            tt(("EL", 0, 256), (EN, 0, 256), ("EH", 0, 256), OP.subtract)
-        for h in range(2):
-            R = (256 * h, 256 * h + 256)
-            mm(("bS%d" % h, 0, 256), [(("ID", 0, 128), ("DC",) + R), (("ID", 0, 128), (LZ,) + R)])
-        for h in range(2):
-            R = (256 * h, 256 * h + 256)
-            ts(("FL",) + R, ("bS%d" % h, 0, 256), 0.5, -0.25, OP.mult, OP.add)
-            emit("v", [lambda e, h=h, R=R: e.tensor_copy(T.D[:, 2048 * h:2048 * h + 2048].indirect(T.LD[:, 16 * h:16 * h + 16]), T.FL[:, R[0]:R[1]])],
-                 [("FL",) + R, ("LD", 16 * h, 16 * h + 16)], [("D", 2048 * h, 2048 * h + 2048)])
+            split(EN, 224, 256, 2)
+        for q, (R, W, C) in enumerate(parts):
+            b = ("bS0", "bS1", "bU0", "bU")[q]
+            extra = [(("ON15", 0, 128), ("K3", 0, SQ))] if q % 2 else []
+            mm((b, 0, SQ), extra + [(("ID", 0, 128), ("DC",) + R), (("ID", 0, 128), (LZ,) + R)])
+            if q % 2:
+                act(("FX", 0, SQ), (b, 0, SQ), AF.Identity, bias=MID, scale=0.5)
+                act(("FB", (q // 2) * SQ, (q // 2) * SQ + SQ), ("FX", 0, SQ), AF.Identity, bias=-MID)
+        for q, (R, W, C) in enumerate(parts):
+            b = ("bS0", "bS1", "bU0", "bU")[q]
+            F = ("FB", (q // 2) * SQ, (q // 2) * SQ + SQ) if q % 2 else ("FL",) + R
+            if q % 2 == 0:
+                ts(F, (b, 0, SQ), 0.5, -0.25, OP.mult, OP.add)
+            emit("v", [lambda e, F=F, W=W, C=C: e.tensor_copy(ap(("D",) + W).indirect(ap(("LD",) + C)), ap(F))],
+                 [F, ("LD",) + C], [("D",) + W])
             if last:
-                ends.append(dma("y", T.yd[:, 2048 * h:2048 * h + 2048], T.D[:, 2048 * h:2048 * h + 2048],
-                                [("D", 2048 * h, 2048 * h + 2048)], [], "sd%d" % h))
+                ends.append(dma("y", T.yd[:, W[0]:W[1]], ap(("D",) + W), [("D",) + W], [], "sd%d" % q))
         if not last:
             spread_first(EN)
         else:
             for h in range(8):
-                mm(("bM", 256 + h, 512, 8), [(("R%d" % h, 7 - k, 135 - k), (e, 32 * k, 32 * k + 32)) for k in range(8) for e in ("EH", "EL")])
-            act(("YE", 0, 256), ("bM", 256, 512), AF.Identity, bias=-1184.0)
+                b, o = ("bM", "bCB")[h // 4], 64 * (h % 4)
+                mm((b, o, o + 64), [(("R%d" % h, 7 - k, 135 - k), ("EHL", 64 * k, 64 * k + 64)) for k in range(8)])
+            for i, b in enumerate(("bM", "bCB")):
+                act(("PK", 128 * i, 128 * i + 128), (b, 0, 256, 2), AF.Identity, bias=-1184.0)
+                for h in range(4):
+                    tt(("YE", 4 * i + h, 256, 8), ("PK", 128 * i + 32 * h, 128 * i + 32 * h + 32), (b, 64 * h + 1, 64 * h + 64, 2), OP.add)
             ends.append(dma("s", T.yz[:, :], T[XN][:, 4096:4608], [(XN, 4096, 4608)], [], "sz"))
             ends.append(dma("s", T.ye[:, :], T.YE[:, :], [("YE", 0, 256)], [], "se"))
     settle("g", ends)

from concourse.mybir import dt, AluOpType, AxisListType, ActivationFunctionType

OP = AluOpType
AF = ActivationFunctionType
RO = 4
BIG = 1.5 * 2.0 ** 35
MID = 1.5 * 2.0 ** 23
SCALE = 4194304.0
B2, B4, I4, U2 = "bfloat16", "float32", "int32", "uint16"
SCRATCH = {}
for _n, _w, _d in (("D", 4096, B2), ("XA0", 4608, B2), ("XA1", 4608, B2), ("XB", 4096, B2), ("GA", 4096, B2), ("GB", 4096, B2),
                   ("GC", 4096, B2), ("DS", 2048, B2), ("DC", 512, B2), ("FL", 512, I4), ("LN", 256, U2), ("LB", 256, U2),
                   ("LC", 256, U2), ("LS", 32, U2), ("LD", 32, U2), ("EQ0", 256, B4), ("EQ1", 256, B4), ("VF", 256, B4), ("PP", 256, B4), ("SI", 256, I4), ("HI", 256, I4), ("NI", 256, I4),
                   ("H0", 256, B4), ("T1", 256, B4), ("PQ", 256, B4), ("PK", 256, B4), ("KEY", 256, B4), ("TR", 256, B4),
                   ("A0T", 32, B4), ("PKS0", 32, I4), ("PKS1", 32, I4), ("TS", 32, I4), ("S0", 32, B2), ("P2", 32, B4),
                   ("ER", 256, B4), ("MK", 256, B4), ("AR", 8, B4), ("AJ", 32, B4), ("NM", 32, I4),
                   ("CI", 32, I4), ("CJ", 32, I4), ("BT", 192, B2), ("BN", 192, B2), ("J8", 32, I4), ("JT", 32, I4),
                   ("ID", 128, B2), ("NG", 128, B2), ("IDF", 128, B4), ("NGF", 128, B4), ("ON15", 128, B2), ("ONS", 128, B2),
                   ("OL", 144, B2), ("WL", 144, B2), ("XI", 144, B4), ("CTI", 256, B4), ("PI", 8, I4), ("PJ", 16, I4),
                   ("PF", 32, B4), ("KM", 16, B4), ("WI", 1, I4), ("WF", 1, B4), ("EFI", 256, I4), ("EF", 256, B4),
                   ("EH", 256, B2), ("EL", 256, B2), ("EHL", 512, B2), ("J4", 32, I4), ("JU", 32, I4), ("K2", 96, B2),
                   ("K3", 256, B2), ("RX", 256, B4), ("RR", 256, B4), ("HP", 256, B2), ("BI", 128, B2), ("FX", 256, B4),
                   ("FB", 256, B2), ("YE", 256, B4)):
    SCRATCH[_n] = ("sbuf", [128, _w], _d)
for _n in ("bU0", "bU", "bCA", "bCB", "bCC", "bS0", "bS1", "bM"):
    SCRATCH[_n] = ("psum", [128, 512], B4)
for _k in range(8):
    SCRATCH["Q%d" % _k] = ("sbuf", [128, 144], B2)
    SCRATCH["R%d" % _k] = ("sbuf", [128, 144], B2)
for _t in range(RO):
    SCRATCH["LP%d" % _t] = ("sbuf", [128, 32], I4)
    SCRATCH["LZ%d" % _t] = ("sbuf", [128, 512], B2)
SEMAPHORES = (["qv", "qs", "qt", "qg"] + ["ldz", "lde", "ldw", "ldd0", "ldd1", "sd0", "sd1", "sd2", "sd3", "se", "sz"]
              + ["%s%d" % (n, t) for t in range(RO) for n in ("an", "az", "ay", "ln", "lz", "ly")])

CFG = {
    "AS": (7, 1, 5),
    "CS": (4, 5),
    "BS": (3, 5),
    "NA": "01 23 45 67", "NC": "123 45 67", "NB": "123 45 67",
    "NU": "12 34 56 7",
    "BM": (1, 6),
    "V": "gaa0 gaa6 gaa3 gaa2 gaa4 sga2 sga6 sga0 sga3 HC sga4 sgc3 sgc6 sgc2 sgc1 sgc7 HB sgb1 sgb2 sgb4 PQ sgb6 sgb7 KEY1 TAIL",
    "S": "gaa7 gaa1 abs7 abs0 sga7 gaa5 abs2 RC abs4 abs1 sga1 abs3 abs6 gac4 abs5 H0 RB sgc4 sga5 gac5 gab3 sgc5 gab5 sgb3 sgb5",
    "T": "sta7 sta1 U7 U0 na6 na2 U1 sta5 na0 U3 stc4 U5 nc1 nc6 na4 stc5 stb3 nc4 stb5 nb1 nb4 nb6",
}


def rank_program(g, core, T, topo):
    rank = T.rank_of(core)
    if rank is None:
        return
    N = len(T.cores)
    AS, CS, BS = CFG["AS"], CFG["CS"], CFG["BS"]
    eng = {"v": g.vector, "s": g.scalar, "t": g.tensor, "g": g, "y": g.sync}
    qsem = {"v": "qv", "s": "qs", "t": "qt", "g": "qg"}
    cnt = {"v": 0, "s": 0, "t": 0, "g": 0}
    known = {q: {} for q in eng}
    log = {}
    BANKS = [b for b in SCRATCH if SCRATCH[b][0] == "psum"]

    def need(q, buf, lo, hi, wr):
        out = []
        for e in log.get(buf, []):
            if e[0] < hi and lo < e[1] and (wr or e[2]):
                out.append(e[4])
            elif buf in BANKS and e[3] != q:
                out.append(e[4])
        return out

    def note(q, buf, lo, hi, wr, op):
        keep = []
        for e in log.get(buf, []):
            covered = lo <= e[0] and e[1] <= hi
            if covered and (wr or (not e[2] and e[3] == q)):
                continue
            keep.append(e)
        keep.append([lo, hi, wr, q, op])
        log[buf] = keep

    def settle(q, ops):
        best = {}
        for op in ops:
            if known[q].get(op[0], 0) < op[1]:
                if op[0] not in best or best[op[0]][1] < op[1]:
                    best[op[0]] = op
        for op in sorted(best.values(), key=lambda o: -len(o[2])):
            if known[q].get(op[0], 0) >= op[1]:
                continue
            eng[q].wait_ge(T.sem[op[0]], op[1])
            for s, v in op[2].items():
                known[q][s] = max(known[q].get(s, 0), v)
            known[q][op[0]] = max(known[q].get(op[0], 0), op[1])

    def emit(q, calls, reads, writes, sem=None, val=None, remote=False):
        ops = []
        for b, lo, hi in reads:
            ops += need(q, b, lo, hi, False)
        for b, lo, hi in writes:
            ops += need(q, b, lo, hi, True)
        settle(q, ops)
        ins = None
        for c in calls:
            ins = c(eng[q])
        snap = dict(known[q])
        if sem is None:
            cnt[q] += 1
            sem, val = qsem[q], cnt[q]
            ins.then_inc(T.sem[sem], 1)
        elif not remote:
            ins.then_inc(T.sem[sem], val)
        snap[sem] = max(snap.get(sem, 0), val)
        op = (sem, val, snap)
        for b, lo, hi in reads:
            note(q, b, lo, hi, False, op)
        for b, lo, hi in writes:
            note(q, b, lo, hi, True, op)
        return op

    def ap(r):
        if len(r) > 3:
            return T[r[0]][:, r[1]:r[2]:r[3]]
        return T[r[0]][:, r[1]:r[2]]

    def reg(r):
        return (r[0], r[1], r[2])

    def copy(out, in_):
        emit("v", [lambda e: e.tensor_copy(ap(out), ap(in_))], [reg(in_)], [reg(out)])

    def tt(out, a, b, op):
        emit("v", [lambda e: e.tensor_tensor(ap(out), ap(a), ap(b), op)], [reg(a), reg(b)], [reg(out)])

    def ts(out, a, s1, s2, op0, op1=None):
        rd = [reg(a)] + [reg(s) for s in (s1, s2) if isinstance(s, tuple)]
        x1 = ap(s1) if isinstance(s1, tuple) else s1
        x2 = ap(s2) if isinstance(s2, tuple) else s2
        if op1 is None:
            emit("v", [lambda e: e.tensor_scalar(ap(out), ap(a), x1, None, op0)], rd, [reg(out)])
        else:
            emit("v", [lambda e: e.tensor_scalar(ap(out), ap(a), x1, x2, op0, op1)], rd, [reg(out)])

    def fill(out, c):
        emit("v", [lambda e: e.memset(ap(out), c)], [], [reg(out)])

    def act(out, in_, func, bias=0.0, scale=1.0):
        rd = [reg(x) for x in (in_, bias, scale) if isinstance(x, tuple)]
        b = ap(bias) if isinstance(bias, tuple) else bias
        k = ap(scale) if isinstance(scale, tuple) else scale
        emit("s", [lambda e: e.activation(ap(out), ap(in_), func, bias=b, scale=k)], rd, [reg(out)])

    def vgather(out, win, off, in1, op):
        emit("v", [lambda e: e.tensor_tensor(ap(out), ap(win).indirect(ap(off)), ap(in1), op)],
             [reg(win), reg(off), reg(in1)], [reg(out)])

    def gcopy(q, out, win, off):
        if q == "v":
            emit("v", [lambda e: e.tensor_copy(ap(out), ap(win).indirect(ap(off)))], [reg(win), reg(off)], [reg(out)])
        else:
            emit("s", [lambda e: e.activation(ap(out), ap(win).indirect(ap(off)), AF.Copy)], [reg(win), reg(off)], [reg(out)])

    def mm(out, parts):
        n = len(parts)
        calls = []
        rd = []
        for i, (l, r) in enumerate(parts):
            rd += [reg(l), reg(r)]
            calls.append(lambda e, l=l, r=r, i=i: e.matmul(ap(out), ap(l), ap(r), i == 0, i == n - 1))
        emit("t", calls, sorted(set(rd)), [reg(out)])

    def wrapped(out, lbuf, rbuf, lo, hi, extra=()):
        mm(out, [((lbuf, 15 - r, 143 - r), (rbuf, lo + r, hi, 16)) for r in range(16)] + list(extra))

    def dma(q, out_ap, in_ap, reads, writes, sem):
        return emit(q, [lambda e: e.dma_start(out=out_ap, in_=in_ap)], reads, writes, sem=sem, val=16)

    def iota(buf, lo, hi, pattern, base, cm, flag):
        if flag:
            emit("g", [lambda e: e.iota(T[buf][:, lo:hi], pattern, base, cm, allow_small_or_imprecise_dtypes=True)], [], [(buf, lo, hi)])
        else:
            emit("g", [lambda e: e.iota(T[buf][:, lo:hi], pattern, base, cm)], [], [(buf, lo, hi)])

    dma("s", T.EFI[:, :], T.ef[:, :], [], [("EFI", 0, 256)], "lde")
    dma("y", T.WI[:, :], T.wt[:, :], [], [("WI", 0, 1)], "ldw")
    dma("y", T.XA0[:, 4096:4608], T.zv[:, :], [], [("XA0", 4096, 4608)], "ldz")
    dma("y", T.D[:, 0:2048], T.dv[:, 0:2048], [], [("D", 0, 2048)], "ldd0")
    dma("s", T.D[:, 2048:4096], T.dv[:, 2048:4096], [], [("D", 2048, 4096)], "ldd1")

    iota("PI", 0, 1, [[1, 1]], 0, 1, False)
    iota("XI", 0, 144, [[1, 144]], 0, 0, True)
    iota("JT", 0, 32, [[128, 32]], 0, 0, False)
    iota("CTI", 32, 256, [[-32, 7], [-1, 32]], 287, 0, True)
    iota("CTI", 0, 32, [[-1, 32]], 31, 0, True)
    I = ("PI", 0, 1)
    ts(("PJ", 0, 1), I, 112, None, OP.bitwise_and)
    ts(("PJ", 1, 2), I, 15, None, OP.bitwise_and)
    ts(("PJ", 2, 3), I, 3, 1, OP.logical_shift_right, OP.bitwise_and)
    ts(("PJ", 3, 4), I, 7, None, OP.bitwise_and)
    ts(("PJ", 4, 5), I, 1, None, OP.bitwise_and)
    ts(("PJ", 5, 6), I, 1, 7, OP.logical_shift_right, OP.bitwise_and)
    copy(("PF", 0, 6), ("PJ", 0, 6))
    copy(("PF", 6, 7), I)
    tt(("PF", 8, 9), ("PF", 0, 1), ("PF", 2, 3), OP.add)
    ts(("PF", 9, 10), ("PF", 8, 9), 14.0, None, OP.add)
    for k in range(8):
        ts(("KM", k, k + 1), ("PF", 3, 4), float(k), None, OP.is_equal)
    for k in range(8):
        ts(("Q%d" % k, 0, 144), ("XI", 0, 144), ("PF", 9, 10), ("KM", k, k + 1), OP.is_equal, OP.mult)
    copy(("EF", 0, 256), ("EFI", 0, 256))

    def split(E, lo, hi, step):
        a = ("EH", lo, hi) if step == 1 else ("EHL", 2 * lo, 2 * hi, 2)
        b = ("EL", lo, hi) if step == 1 else ("EHL", 2 * lo + 1, 2 * hi, 2)
        copy(a, (E, lo, hi))
        tt(b, (E, lo, hi), a, OP.subtract)
    split("EF", 0, 256, 1)

    def bring(b, k):
        mm((b, 32 * k, 32 * k + 32), [(("Q%d" % k, 14 - 2 * h, 142 - 2 * h), (e, h, 256, 8)) for h in range(8) for e in ("EH", "EL")])
    for k in range(4):
        bring("bCA", k)
    ts(("PF", 10, 11), ("PF", 0, 1), 15.0, None, OP.add)
    ts(("OL", 0, 144), ("XI", 0, 144), ("PF", 10, 11), SCALE, OP.is_equal, OP.mult)
    copy(("WF", 0, 1), ("WI", 0, 1))
    ts(("WL", 0, 144), ("XI", 0, 144), ("PF", 10, 11), ("WF", 0, 1), OP.is_equal, OP.mult)
    ts(("ID", 0, 128), ("XI", 0, 128), ("PF", 6, 7), None, OP.is_equal)
    ts(("NG", 0, 128), ("XI", 0, 128), ("PF", 6, 7), -1.0, OP.is_equal, OP.mult)
    ts(("IDF", 0, 128), ("XI", 0, 128), ("PF", 6, 7), None, OP.is_equal)
    ts(("NGF", 0, 128), ("XI", 0, 128), ("PF", 6, 7), -1.0, OP.is_equal, OP.mult)
    fill(("BT", 0, 96), -7.5)
    fill(("BT", 96, 192), 1.0)
    fill(("BN", 0, 96), -1.0)
    fill(("BN", 96, 192), -2.0)
    fill(("ON15", 0, 128), SCALE / 128)
    fill(("K2", 0, 96), 2048 / SCALE)
    fill(("K3", 0, 256), -0.5 / SCALE)
    ts(("BI", 0, 128), ("XI", 0, 128), ("PF", 6, 7), 64 * SCALE, OP.is_equal, OP.mult)
    fill(("ONS", 0, 128), 2.0 ** -21)
    ts(("PF", 11, 12), ("PF", 1, 2), 4592.0, None, OP.add)
    ts(("PF", 12, 13), ("PF", 1, 2), 8.0, None, OP.mult)
    for j, m in (("J8", 2047), ("J4", 1023)):
        ts(("JU", 0, 32), ("JT", 0, 32), m, None, OP.bitwise_and)
        ts((j, 0, 32), ("JU", 0, 32), ("PF", 12, 13), None, OP.add)
    ts(("PF", 13, 14), ("PF", 4, 5), 8.0, 7.0, OP.mult, OP.add)
    tt(("PF", 14, 15), ("PF", 13, 14), ("PF", 0, 1), OP.add)
    for h in range(8):
        ts(("KM", 8 + h, 9 + h), ("PF", 5, 6), float(h), None, OP.is_equal)
        ts(("R%d" % h, 0, 144), ("XI", 0, 144), ("PF", 14, 15), ("KM", 8 + h, 9 + h), OP.is_equal, OP.mult)

    def second(EQ, lo, hi):
        act(("bU0", lo, hi), (EQ, lo, hi), AF.Identity, bias=-6722560.0, scale=2080.0)

    def spread_first(EQ):
        act(("ER", 0, 32), (EQ, 0, 32), AF.Copy)
        act(("ER", 32, 64), (EQ, 0, 32), AF.Copy)
        act(("ER", 64, 128), ("ER", 0, 64), AF.Copy)
        act(("ER", 128, 224), ("ER", 0, 96), AF.Copy)
        act(("bU0", 256, 480), ("ER", 0, 224), AF.Copy)
        act(("bU", 288, 512), ("ER", 0, 224), AF.Identity, bias=-6722560.0, scale=2080.0)

    def round_s(src, lo):
        n = src[2] - src[1]
        act(("RX", lo, lo + n), src, AF.Identity, bias=BIG, scale=1.0 + 2.0 ** -22)
        act(("RR", lo, lo + n), ("RX", lo, lo + n), AF.Identity, bias=-BIG)

    def value_v(src, lo):
        n = src[2] - src[1]
        tt(("VF", lo, lo + n), src, ("RR", lo, lo + n), OP.subtract)

    def finish(lo, hi, ni, lst):
        ts((ni, lo, hi), ("SI", lo, hi), 5, 4095, OP.arith_shift_right, OP.bitwise_and)
        copy((lst, lo, hi), (ni, lo, hi))

    def hash_many(EQ, k0, k1, ni, lst):
        products(EQ, k0, k1)
        names(k0, k1, ni, lst)

    def products(EQ, k0, k1):
        for k in range(k0, k1):
            tt(("PP", 32 * k, 32 * k + 32), (EQ, 32 * k, 32 * k + 32), ("VF", 0, 32), OP.mult)

    def names(k0, k1, ni, lst):
        tt(("SI", 32 * k0, 32 * k1), ("PP", 32 * k0, 32 * k1), ("bU0", 32 * k0, 32 * k1), OP.add)
        finish(32 * k0, 32 * k1, ni, lst)

    def hash_first():
        tt(("PP", 32, 256), ("bU0", 256, 480), ("VF", 32, 256), OP.mult)
        tt(("SI", 32, 256), ("PP", 32, 256), ("bU", 288, 512), OP.add)
        finish(32, 256, "HI", "LB")

    def uz(XA):
        wrapped(("bU", 256, 288), "WL", XA, 4096, 4608, [(("ON15", 0, 128), ("K2", 0, 32))])

    uz("XA0")
    for k in range(4, 8):
        bring("bCB", k)
    act(("bCC", 256, 512), ("CTI", 0, 256), AF.Copy, scale=4096.0)
    for h, b in ((0, "bCA"), (1, "bCB")):
        act(("EQ0", 128 * h, 128 * h + 128), (b, 128 * h, 128 * h + 128), AF.Identity, bias=1184.0)
        second("EQ0", 128 * h, 128 * h + 128)
        if h == 0:
            round_s(("bU", 256, 288), 0)
            value_v(("bU", 256, 288), 0)
        hash_many("EQ0", 4 * h, 4 * h + 4, "NI", "LN")
    spread_first("EQ0")

    def packs():
        tt(("PK", 0, 256), ("NI", 0, 256), ("bCC", 256, 512), OP.add)
    packs()

    ends = []
    for t in range(RO):
        last = t == RO - 1
        XA, XN = "XA%d" % (t % 2), "XA%d" % ((t + 1) % 2)
        EQ, EN = "EQ%d" % (t % 2), "EQ%d" % ((t + 1) % 2)
        PKS = "PKS%d" % (t % 2)
        ZB = (XA, 4096, 4608)
        DW = ("D", 0, 4096)
        tasks = {}
        order = ["a%d" % k for k in AS] + ["c%d" % k for k in CS] + ["b%d" % k for k in BS]

        def add(name, q, pre, fn):
            tasks[name] = (q, pre, fn)

        def xa(k):
            b = (k - 1) % 8
            return (XA, 512 * b, 512 * b + 512)

        def lst(name, k):
            return (name, 32 * k, 32 * k + 32)

        def blk(name, k):
            return (name, 512 * k, 512 * k + 512)

        def bank(name):
            return ("bS%d" % (order.index(name) % 2), 0, 512)

        def ds(name):
            i = order.index(name) % 4
            return ("DS", 512 * i, 512 * i + 512)

        def by_scalar(n, pre, L, k, y, G, extra):
            i = order.index(n)
            add("ga" + n, "s", pre, lambda: gcopy("s", ds(n), DW, lst(L, k)))
            add("st" + n, "t", ["ga" + n] + (["sg" + order[i - 2]] if i >= 2 else []),
                lambda: mm(bank(n), [(("ID", 0, 128), ds(n)), (("NG", 0, 128), y)]))
            add("sg" + n, "s", ["st" + n] + extra, lambda: act(blk(G, k), bank(n), AF.Sign, bias=-0.5))
        for k in range(8):
            if k in AS:
                n = "a%d" % k
                add("abs%d" % k, "s", ["st" + n], lambda n=n, k=k: act(xa(k), bank(n), AF.Abs))
                by_scalar(n, [], "LN", k, ZB, "GA", ["abs%d" % k])
            else:
                add("gaa%d" % k, "v", [], lambda k=k: vgather(blk("XB", k), DW, lst("LN", k), ZB, OP.subtract))
                add("abs%d" % k, "s", ["gaa%d" % k], lambda k=k: act(xa(k), blk("XB", k), AF.Abs))
                add("sga%d" % k, "v", ["gaa%d" % k], lambda k=k: ts(blk("GA", k), blk("XB", k), 0.0, None, OP.is_gt))
            for w, S_, G, L, pre in (("c", CS, "GC", "LC", "HC"), ("b", BS, "GB", "LB", "HB")):
                if k == 0:
                    continue
                n = w + str(k)
                y = xa(0) if w == "c" else xa(k)
                if k in S_:
                    by_scalar(n, [pre], L, k, y, G, [])
                elif w == "b" and k in CFG["BM"]:
                    add("sg" + n, "v", [pre], lambda k=k: vgather(("GB", 512 * k, 512 * k + 1024), DW, ("LB", 32 * k, 32 * k + 64),
                                                                  (XA, 512 * k - 512, 512 * k + 512), OP.is_gt))
                elif w == "b" and k - 1 in CFG["BM"]:
                    add("sg" + n, "v", ["sgb%d" % (k - 1)], lambda: None)
                else:
                    add("sg" + n, "v", [pre], lambda k=k, G=G, L=L, y=y: vgather(blk(G, k), DW, lst(L, k), y, OP.is_gt))

        def count(w, ks):
            G, B, S_ = {"a": ("GA", "bCA", AS), "b": ("GB", "bCB", BS), "c": ("GC", "bCC", CS)}[w]
            kinds = [k in S_ for k in ks]
            k0, n = ks[0], len(ks)
            if kinds == sorted(kinds):
                b0 = 96 - 32 * kinds.count(False)
                o = 32 * k0
                if w == "b" and k0 >= 6:
                    B, o = "bM", 32 * k0 + 128
                extra = [(("ON15", 0, 128), ("BT", b0, b0 + 32 * n))]
                if w == "c":
                    extra.append((("BI", 0, 128), ("HP", 32 * k0, 32 * (k0 + n))))
                wrapped((B, o, o + 32 * n), "OL", G, 512 * k0, 512 * (k0 + n), extra)
            else:
                for k in ks:
                    count(w, [k])
        for w, c in (("a", "NA"), ("c", "NC"), ("b", "NB")):
            for grp in CFG[c].split():
                ks = [int(x) for x in grp]
                add("n%s%d" % (w, ks[0]), "t", ["sg%s%d" % (w, k) for k in ks] + (["H0"] if w == "c" else []), lambda w=w, ks=ks: count(w, ks))
        counts = ["n%s%s" % (w, grp[0]) for w, c in (("a", "NA"), ("c", "NC")) for grp in CFG[c].split()]
        late = "nb" + CFG["NB"].split()[-1][0]
        add("U0", "t", ["abs0"], lambda: wrapped(("bM", 288, 320), "WL", XA, 3584, 4096, [(("ON15", 0, 128), ("K2", 0, 32))]))
        add("RC", "s", ["U0"], lambda: round_s(("bM", 288, 320), 0))
        UG = [[int(x) for x in grp] for grp in CFG["NU"].split()]
        for ks in UG:
            add("U%d" % ks[0], "t", ["abs%d" % k for k in ks], lambda ks=ks: wrapped(
                ("bU", 32 * ks[0], 32 * ks[-1] + 32), "WL", XA, 512 * (ks[0] - 1), 512 * ks[-1],
                [(("ON15", 0, 128), ("K2", 0, 32 * len(ks)))]))

        def do_par():
            emit("s", [lambda e: e.activation(T.AJ[:, 0:32], T.bM[:, 256:288], AF.Copy, accum_out=T.AR[:, 0:1])],
                 [("bM", 256, 288)], [("AJ", 0, 32), ("AR", 0, 1)])
            act(("AR", 1, 2), ("AR", 0, 1), AF.Identity, bias=MID, scale=0.5)
            act(("AR", 2, 3), ("AR", 1, 2), AF.Identity, bias=2 * MID, scale=-2.0)
            act(("AR", 3, 4), ("AR", 2, 3), AF.Abs, bias=("AR", 0, 1))
            for lo, b in ((0, -7.5), (96, 1.0)):
                act(("BT", lo, lo + 96), ("BN", lo, lo + 96), AF.Identity, bias=b, scale=("AR", 3, 4))

        def do_hc():
            value_v(("bM", 288, 320), 0)
            hash_many(EQ, 1, 8, "HI", "LC")
        add("HC", "v", ["RC"], do_hc)

        def do_rb():
            round_s(("bU", 32, 256), 32)
        add("RB", "s", ["U%d" % ks[0] for ks in UG], do_rb)

        def do_hb():
            value_v(("bU", 32, 256), 32)
            hash_first()
        add("HB", "v", ["RB", "HC"], do_hb)

        def do_h0():
            for k in range(1, 8):
                act(("H0", 32 * k, 32 * k + 32), ("bCA", 0, 32), AF.Copy, scale=-1.0)
            act(("HP", 32, 256), ("H0", 32, 256), AF.Relu, scale=1.0 / SCALE)
        add("H0", "s", ["na0"], do_h0)

        def do_pq():
            ts(("A0T", 0, 32), ("bCA", 0, 32), 0.0, 131072.0, OP.is_gt, OP.mult)
            tt(("T1", 32, 256), ("bCC", 32, 256), ("PK", 32, 256), OP.min)
            tt(("KEY", 0, 32), ("PK", 0, 32), ("A0T", 0, 32), OP.add)
            tt(("PQ", 32, 256), ("bCA", 32, 256), ("T1", 32, 256), OP.min)
        add("PQ", "v", ["H0"] + counts, do_pq)

        def key(lo, hi):
            cb = ("bCB", lo, hi) if lo < 192 else ("bM", lo + 128, hi + 128)
            tt(("bCA", 256 + lo, 256 + hi), cb, ("H0", lo, hi), OP.mult)
            tt(("KEY", lo, hi), ("PQ", lo, hi), ("bCA", 256 + lo, 256 + hi), OP.min)

        def do_key1():
            key(32, 192)
            tt(("TR", 0, 96), ("KEY", 0, 96), ("KEY", 96, 192), OP.max)
            tt(("TR", 96, 128), ("TR", 0, 32), ("TR", 32, 64), OP.max)
            tt(("TR", 128, 160), ("TR", 96, 128), ("TR", 64, 96), OP.max)
        add("KEY1", "v", ["PQ"] + ["nb" + grp[0] for grp in CFG["NB"].split()[:-1]], do_key1)

        def do_tail():
            key(192, 256)
            tt(("TR", 160, 192), ("KEY", 192, 224), ("KEY", 224, 256), OP.max)
            tt((PKS, 0, 32), ("TR", 128, 160), ("TR", 160, 192), OP.max)
            ts(("TS", 0, 32), (PKS, 0, 32), 12, None, OP.arith_shift_right)
            ts(("LS", 0, 32), ("TS", 0, 32), -16.0, ("PF", 11, 12), OP.mult, OP.add)
        add("TAIL", "v", ["KEY1", late], do_tail)

        lists = {"v": CFG["V"].split(), "s": CFG["S"].split(), "t": CFG["T"].split()}
        assert sorted(lists["v"] + lists["s"] + lists["t"]) == sorted(tasks), set(tasks) ^ set(lists["v"] + lists["s"] + lists["t"])
        done = set()
        pos = {"v": 0, "s": 0, "t": 0}
        while len(done) < len(tasks):
            moved = False
            for q in ("v", "s", "t"):
                while pos[q] < len(lists[q]) and all(p in done for p in tasks[lists[q][pos[q]]][1]):
                    nm = lists[q][pos[q]]
                    assert tasks[nm][0] == q
                    tasks[nm][2]()
                    done.add(nm)
                    pos[q] += 1
                    moved = True
            assert moved, [lists[q][pos[q]:pos[q] + 1] for q in lists]

        mm(("bCB", 256, 480), [(("IDF", 0, 128), (EQ, 32, 256)), (("NGF", 0, 128), (EQ, 0, 224))])

        dst = T.cores[(rank + 1 + t % (N - 1)) % N]
        rid, pid = topo.addr(dst)[0], topo.addr(dst)[1]
        mask = topo.mask(core, dst)
        ne = len(topo.engines(core, dst))

        def send(out, in_, rsem, lsem):
            return emit("g", [lambda e: e.remote_dma(ap(out), ap(in_), T.sem[rsem], T.sem[lsem], pid, rid, mask)],
                        [reg(in_)], [], sem=lsem, val=ne, remote=True)

        def landed(buf, lo, hi, rsem):
            note("g", buf, lo, hi, True, (rsem, ne, {rsem: ne}))
        LP, LZ = "LP%d" % t, "LZ%d" % t
        ends.append(send((LP, 0, 32), (PKS, 0, 32), "an%d" % t, "ln%d" % t))
        gcopy("v", (XN, 4096, 4352), (XA, 0, 4608), ("LS", 0, 16))
        gcopy("s", (XN, 4352, 4608), (XA, 0, 4608), ("LS", 16, 32))
        ends.append(send((LZ, 0, 256), (XN, 4096, 4352), "az%d" % t, "lz%d" % t))
        ends.append(send((LZ, 256, 512), (XN, 4352, 4608), "ay%d" % t, "ly%d" % t))
        landed(LP, 0, 32, "an%d" % t)
        landed(LZ, 0, 256, "az%d" % t)
        landed(LZ, 256, 512, "ay%d" % t)

        ts(("S0", 0, 32), (PKS, 0, 32), 262144.0, 2097152.0, OP.is_lt, OP.mult)
        tt(("P2", 0, 32), (PKS, 0, 32), ("S0", 0, 32), OP.add)
        if not last:
            mm(("bM", 256, 288), [(("ONS", 0, 128), ("S0", 0, 32))])
        for k in range(7):
            ts(("MK", 32 * k, 32 * k + 32), ("P2", 0, 32), float((9 - k) * 131072), None, OP.is_ge)
        if not last:
            uz(XN)
            round_s(("bU", 256, 288), 0)
        tt(("bCB", 256, 480), ("bCB", 256, 480), ("MK", 0, 224), OP.mult)
        tt((EN, 0, 224), ("bCB", 256, 480), (EQ, 0, 224), OP.add)
        if not last:
            second(EN, 0, 224)
            value_v(("bU", 256, 288), 0)
            do_par()
            products(EN, 0, 7)
        else:
            split(EN, 0, 224, 2)
        J, nq = ("J4", 4) if last else ("J8", 2)
        ts(("NM", 0, 32), (LP, 0, 32), 4095, None, OP.bitwise_and)
        ts(("CI", 0, 32), (LP, 0, 32), 7, None, OP.bitwise_and)
        ts((EN, 224, 256), ("NM", 0, 32), 1184.0, None, OP.add)
        tt(("CJ", 0, 32), ("CI", 0, 32), (J, 0, 32), OP.add)
        copy(("LD", 0, 32), ("CJ", 0, 32))
        if not last:
            second(EN, 224, 256)
        WQ, SQ, CQ = 4096 // nq, 512 // nq, 32 // nq
        parts = [((SQ * q, SQ * q + SQ), (WQ * q, WQ * q + WQ), (CQ * q, CQ * q + CQ)) for q in range(nq)]
        for q, (R, W, C) in enumerate(parts):
            gcopy("s", ("DC",) + R, ("D",) + W, ("LD",) + C)
        if not last:
            products(EN, 7, 8)
            names(0, 8, "NI", "LN")
            packs()
        else:
            split(EN, 224, 256, 2)
        for q, (R, W, C) in enumerate(parts):
            b = ("bS0", "bS1", "bU0", "bU")[q]
            extra = [(("ON15", 0, 128), ("K3", 0, SQ))] if q % 2 else []
            mm((b, 0, SQ), extra + [(("ID", 0, 128), ("DC",) + R), (("ID", 0, 128), (LZ,) + R)])
            if q % 2:
                act(("FX", 0, SQ), (b, 0, SQ), AF.Identity, bias=MID, scale=0.5)
                act(("FB", (q // 2) * SQ, (q // 2) * SQ + SQ), ("FX", 0, SQ), AF.Identity, bias=-MID)
        for q, (R, W, C) in enumerate(parts):
            b = ("bS0", "bS1", "bU0", "bU")[q]
            F = ("FB", (q // 2) * SQ, (q // 2) * SQ + SQ) if q % 2 else ("FL",) + R
            if q % 2 == 0:
                ts(F, (b, 0, SQ), 0.5, -0.25, OP.mult, OP.add)
            emit("v", [lambda e, F=F, W=W, C=C: e.tensor_copy(ap(("D",) + W).indirect(ap(("LD",) + C)), ap(F))],
                 [F, ("LD",) + C], [("D",) + W])
            if last:
                ends.append(dma("y", T.yd[:, W[0]:W[1]], ap(("D",) + W), [("D",) + W], [], "sd%d" % q))
        if not last:
            spread_first(EN)
        else:
            for h in range(8):
                b, o = ("bM", "bCB")[h // 4], 64 * (h % 4)
                mm((b, o, o + 64), [(("R%d" % h, 7 - k, 135 - k), ("EHL", 64 * k, 64 * k + 64)) for k in range(8)])
            for i, b in enumerate(("bM", "bCB")):
                act(("PK", 128 * i, 128 * i + 128), (b, 0, 256, 2), AF.Identity, bias=-1184.0)
                for h in range(4):
                    tt(("YE", 4 * i + h, 256, 8), ("PK", 128 * i + 32 * h, 128 * i + 32 * h + 32), (b, 64 * h + 1, 64 * h + 64, 2), OP.add)
            ends.append(dma("s", T.yz[:, :], T[XN][:, 4096:4608], [(XN, 4096, 4608)], [], "sz"))
            ends.append(dma("s", T.ye[:, :], T.YE[:, :], [("YE", 0, 256)], [], "se"))
    settle("g", ends)
    settle("g", [(qsem[q], cnt[q], {}) for q in "vstg"])
